import numpy as np
import ml_dtypes


def mxq(x, axis, fmt="e4m3"):
    dtype, down = {"e4m3": (ml_dtypes.float8_e4m3fn, 7), "e5m2": (ml_dtypes.float8_e5m2, 14)}[fmt]
    v = np.moveaxis(np.asarray(x, np.float32).astype(ml_dtypes.bfloat16).astype(np.float64), axis, -1)
    blocks = v.reshape(v.shape[:-1] + (-1, 32))
    amax = np.abs(blocks).max(-1, keepdims=True)
    byte = np.maximum(np.where(amax > 0, np.frexp(amax)[1] - 1 + 127, 0) - down, 1)
    scale = np.exp2(byte - 127.0)
    codes = (blocks / scale).astype(np.float32).astype(dtype).astype(np.float64)
    return np.moveaxis((codes * scale).reshape(v.shape), -1, axis)


WIDE = False


def mx_kscale(k):
    if not WIDE:
        return np.ones(k)
    levels = np.array([10, -10, 5, -5, 0])
    if k % 512:
        return np.exp2(np.random.permutation(np.resize(levels, k // 32))).repeat(32)
    a = np.empty((k // 512, 16))
    for p in range(k // 512):
        a[p, :8] = np.random.permutation(np.resize(levels, 8))
        for g in range(8):
            far = levels[np.abs(levels - a[p, g]) >= 10]
            a[p, g + 8] = far[np.random.randint(len(far))]
    return np.exp2(a.ravel()).repeat(32)


def f64(x):
    return np.asarray(x).astype(np.float64)


def striped(idx):
    return np.tile(idx.reshape(-1, 16).T, (8, 1)).astype(np.uint16)


def unstriped(offs):
    return offs[:16].T.reshape(-1).astype(np.int64)


E2M1 = np.array([0.0, 0.5, 1.0, 1.5, 2.0, 3.0, 4.0, 6.0, -0.0, -0.5, -1.0, -1.5, -2.0, -3.0, -4.0, -6.0])


def pack_weight(w, fmt):
    k, n = w.shape
    w = f64(np.asarray(w, np.float32).astype(ml_dtypes.bfloat16)).reshape(k // 32, 32, n)
    amax = np.abs(w).max(1)
    if fmt == "e4m3":
        byte = np.frexp(amax)[1] - 1 + 127 - 7
    else:
        mant, ex = np.frexp(amax / 6.0)
        byte = np.where(mant > 0.5, ex, ex - 1) + 127
    byte = np.clip(np.where(amax > 0, byte, 1), 1, 254)
    scaled = (w * np.exp2(127.0 - byte)[:, None, :]).reshape(k, n).astype(np.float32)
    by_word = np.ascontiguousarray(scaled.reshape(k // 512, 128, 4, n).transpose(0, 1, 3, 2))
    if fmt == "e4m3":
        words = by_word.astype(ml_dtypes.float8_e4m3fn).view(np.uint8)
    else:
        c = by_word.astype(ml_dtypes.float4_e2m1fn).view(np.uint8) & 0xF
        words = (c[..., 0::2] | (c[..., 1::2] << 4)).reshape(k // 512, 128, 2 * n)
    return np.ascontiguousarray(words), np.ascontiguousarray(byte.astype(np.uint8).reshape(k // 512, 16, n))


def unpack_weight(words, scales, fmt):
    g, _, n = scales.shape
    words = np.ascontiguousarray(words).reshape(g, 128, n, -1)
    if fmt == "e4m3":
        vals = words.view(ml_dtypes.float8_e4m3fn).astype(np.float64)
    else:
        nib = np.empty((g, 128, n, 4), np.uint8)
        nib[..., 0::2] = words & 0xF
        nib[..., 1::2] = words >> 4
        vals = E2M1[nib]
    vals = vals * np.repeat(np.exp2(scales.astype(np.float64) - 127.0), 8, axis=1)[..., None]
    return vals.transpose(0, 1, 3, 2).reshape(g * 512, n)


def split(x):
    m, e = np.frexp(f64(x))
    hi = np.ldexp(np.trunc(16.0 * m) / 16.0, e)
    return hi, f64(x) - hi


def gelu(v):
    return 0.5 * v * (1.0 + np.tanh(np.sqrt(2.0 / np.pi) * (v + 0.044715 * v**3)))


K, M, T, S = 1536, 512, 4096, 2048


def setup_inputs():
    n = np.random.standard_normal
    s = mx_kscale(K)[:, None]
    v = pack_weight(n((K, T)) * s, "e4m3")
    return {
        "tab_words": v[0],
        "tab_scales": v[1],
        "w": (n((K, M)) / np.sqrt(K) / s).astype(np.float32),
        "gT": n((M, T)).astype(np.float32),
        "b": (0.3 * n(512)).astype(np.float32),
        "offs": striped(np.random.permutation(T)[:S]),
    }


def reference(tab_words, tab_scales, w, gT, b, offs):
    tab_ = unpack_weight(tab_words, tab_scales, "e4m3")[:, unstriped(offs)]
    w_hi, w_lo = split(w)
    w_hi_, w_lo_ = mxq(w_hi, 0, "e4m3"), mxq(w_lo, 0, "e4m3")
    y = w_hi_.T @ tab_ + w_lo_.T @ tab_
    return (gelu(y + f64(b)[:, None])) * f64(gT)[:, unstriped(offs)]

@@ -1,0 +1,172 @@
+from contextlib import ExitStack
+
+import concourse.mybir as mybir
+
+K, M, T, S = 1536, 512, 4096, 2048
+FLOPS = 2 * 2 * K * M * S
+
+F32 = mybir.dt.float32
+BF16 = mybir.dt.bfloat16
+I32 = mybir.dt.int32
+U32 = mybir.dt.uint32
+U16 = mybir.dt.uint16
+U8 = mybir.dt.uint8
+FP8X4 = mybir.dt.float8_e4m3fn_x4
+ALU = mybir.AluOpType
+GELU = mybir.ActivationFunctionType.Gelu_apprx_tanh
+
+P = 128
+PACK = 4
+PASSES = K // (P * PACK)
+HALF = M // 2
+BANK = 512
+HI_MASK = 0xFFF0FFF0 - (1 << 32)
+
+
+def tile_list_tabgate_gelu_kernel(tc, tab_words, tab_scales, w, gT, b, offs, out):
+    nc = tc.nc
+    with ExitStack() as ctx:
+        keep = ctx.enter_context(tc.tile_pool(name="keep", bufs=1))
+        ring = ctx.enter_context(tc.tile_pool(name="ring", bufs=2))
+        psum = ctx.enter_context(tc.psum_pool(name="psum", bufs=8))
+
+        offsets = keep.tile([P, S // 16], U16, name="offsets")
+        nc.sync.dma_start(offsets[:], offs)
+
+        def picks(start, count):
+            return offsets[:, start // 16 : (start + count) // 16]
+
+        plane = keep.tile([P, T // 4], I32, name="plane")
+        nc.vector.memset(plane[:], 0)
+        w_raw, table, gates = {}, {}, []
+
+        def load_weights(a, first, count):
+            rows = w[512 * a : 512 * (a + 1), :].rearrange("(p t) n -> p t n", t=PACK)
+            piece = keep.tile([P, PACK, count * P], F32, name="w_raw%d_%d" % (a, first))
+            nc.sync.dma_start(piece[:], rows[:, :, first * P : (first + count) * P])
+            for m in range(first, first + count):
+                w_raw[a, m] = (piece, (m - first) * P)
+
+        def load_table(a):
+            table[a] = keep.tile([P, T], I32, name="table%d" % a)
+            nc.sync.dma_start(table[a][:], tab_words[a].rearrange("p t i -> p (t i)").bitcast(I32))
+
+        load_weights(0, 0, 1)
+        load_weights(0, 1, 1)
+        load_weights(0, 2, 2)
+        load_weights(1, 0, 4)
+        bias = keep.tile([P, M // P], F32, name="bias")
+        with nc.allow_non_contiguous_dma(reason="one bias value a partition"):
+            nc.sync.dma_start(bias[:], b.rearrange("(c p) -> p c", p=P))
+        for a in range(PASSES):
+            for q in range(4):
+                row = 32 * q + 4 * a
+                nc.sync.dma_start(plane[row : row + 4, :], tab_scales[a, 4 * q : 4 * q + 4, :].bitcast(I32))
+        load_table(0)
+        load_table(1)
+        load_weights(2, 0, 4)
+        load_table(2)
+        for m in range(M // P):
+            gates.append(keep.tile([P, T], F32, name="gates%d" % m))
+            nc.sync.dma_start(gates[m][:], gT[P * m : P * (m + 1), :])
+
+        picked_scales = keep.tile([P, S], U8, name="picked_scales", align_bytes=64)
+        picked_words = [keep.tile([P, S], U32, name="picked_words%d" % a, align_bytes=64) for a in range(PASSES)]
+        weights = {}
+
+        def gather_scales(start, count):
+            nc.vector.tensor_copy(picked_scales[:, start : start + count], plane[:].bitcast(U8).indirect(picks(start, count)))
+
+        def gather_words(a, start, count):
+            nc.vector.tensor_copy(picked_words[a][:, start : start + count], table[a][:].bitcast(U32).indirect(picks(start, count)))
+
+        def grouped(ap):
+            return ap.rearrange("p (c i t) -> p c t i", i=4, t=PACK)
+
+        def split_weights(a, first, count):
+            width = count * P
+            piece, col = w_raw[a, first]
+            blocks = slice(col // 4, (col + width) // 4)
+            upper = ring.tile([P, width * PACK], BF16, name="upper")
+            halves = piece[:].bitcast(BF16).rearrange("p t (c i two) -> p c t i two", i=4, two=2)
+            nc.scalar.copy(grouped(upper[:]), halves[:, blocks, :, :, 1])
+            parts = ring.tile([P, 2, width * PACK], BF16, name="parts", align_bytes=64, bufs=3)
+            nc.vector.tensor_scalar(parts[:, 0, :].bitcast(I32), upper[:].bitcast(I32), HI_MASK, None, ALU.bitwise_and)
+            whole = piece[:].rearrange("p t (c i) -> p c t i", i=4)
+            nc.vector.tensor_tensor(grouped(parts[:, 1, :]), whole[:, blocks, :, :], grouped(parts[:, 0, :]), ALU.subtract)
+            codes = keep.tile([P, 2, width], U32, name="codes%d_%d" % (a, first), align_bytes=64)
+            scales = keep.tile([P, 2, width], U8, name="scales%d_%d" % (a, first), align_bytes=64)
+            nc.vector.quantize_mx(
+                codes[:].rearrange("p s n -> p (s n)").bitcast(FP8X4),
+                scales[:].rearrange("p s n -> p (s n)"),
+                parts[:].rearrange("p s x -> p (s x)"),
+            )
+            for m in range(first, first + count):
+                weights[a, m] = (codes, scales, slice((m - first) * P, (m - first + 1) * P))
+
+        def multiply(acc, a, m, s):
+            codes, scales, wcols = weights[a, m]
+            cols = slice(s * BANK, (s + 1) * BANK)
+            for part in range(2):
+                nc.tensor.matmul_mx(
+                    out=acc[:],
+                    lhsT=codes[:, part, wcols].bitcast(FP8X4),
+                    lhsT_scale=scales[:, part, wcols],
+                    rhs=picked_words[a][:, cols].bitcast(FP8X4),
+                    rhs_scale=picked_scales[4 * a :, cols],
+                    start=(a == 0 and part == 0),
+                    stop=(a == PASSES - 1 and part == 1),
+                )
+
+        acts = {}
+
+        def activate(acc, m, s):
+            if s % 2 == 0:
+                acts[m, s // 2] = ring.tile([P, 2 * BANK], F32, name="act", bufs=4)
+            nc.scalar.activation(acts[m, s // 2][:, (s % 2) * BANK : (s % 2 + 1) * BANK], acc[:], GELU, bias=bias[:, m : m + 1])
+
+        def gate(m, start, count):
+            act = acts[m, start // (2 * BANK)]
+            lo = start % (2 * BANK)
+            result = ring.tile([P, count], F32, name="result", bufs=4)
+            nc.vector.tensor_tensor(result[:], gates[m][:].indirect(picks(start, count)), act[:, lo : lo + count], ALU.mult)
+            nc.sync.dma_start(out[P * m : P * (m + 1), start : start + count], result[:])
+
+        accs = {}
+        split_weights(0, 0, 1)
+        split_weights(0, 1, 1)
+        split_weights(0, 2, 2)
+        split_weights(1, 0, 2)
+        split_weights(1, 2, 2)
+        gather_scales(0, S)
+        for a in range(PASSES):
+            if a == PASSES - 1:
+                split_weights(a, 0, 2)
+            step = 1024 if a < PASSES - 1 else 512
+            for start in range(0, S, step):
+                gather_words(a, start, step)
+                for s in range(start // BANK, (start + step) // BANK):
+                    for m in range(2):
+                        if a == 0:
+                            accs[m, s] = psum.tile([P, BANK], F32, name="acc")
+                        multiply(accs[m, s], a, m, s)
+        split_weights(PASSES - 1, 2, 2)
+        for half in range(2):
+            for m in range(2):
+                for s in (2 * half, 2 * half + 1):
+                    activate(accs[m, s], m, s)
+        for m in range(2, 4):
+            for s in range(S // BANK):
+                accs[m, s] = psum.tile([P, BANK], F32, name="acc")
+                for a in range(PASSES):
+                    multiply(accs[m, s], a, m, s)
+        for start in range(0, S, 1024):
+            for m in range(2):
+                gate(m, start, 1024)
+        for m in range(2, 4):
+            for s in range(S // BANK):
+                activate(accs[m, s], m, s)
+            start = 0
+            for count in (1024, 1024) if m == 2 else (1024, 512, 256, 256):
+                gate(m, start, count)
+                start += count

@@ -18,7 +18,6 @@ GELU = mybir.ActivationFunctionType.Gelu_apprx_tanh
 P = 128
 PACK = 4
 PASSES = K // (P * PACK)
-HALF = M // 2
 BANK = 512
 HI_MASK = 0xFFF0FFF0 - (1 << 32)
 
@@ -36,35 +35,36 @@ def tile_list_tabgate_gelu_kernel(tc, tab_words, tab_scales, w, gT, b, offs, out
         def picks(start, count):
             return offsets[:, start // 16 : (start + count) // 16]
 
-        plane = keep.tile([P, T // 4], I32, name="plane")
+        plane = keep.tile([P, T // 4], I32, name="plane", tag="plane", align_bytes=64)
         nc.vector.memset(plane[:], 0)
+        warm = keep.tile([P, 2], F32, name="warm")
+        nc.gpsimd.memset(warm[:, 0:1], 0.0)
+        nc.scalar.activation(warm[:, 1:2], warm[:, 0:1], GELU)
+
         w_raw, table, gates = {}, {}, []
 
         def load_weights(a, first, count):
             rows = w[512 * a : 512 * (a + 1), :].rearrange("(p t) n -> p t n", t=PACK)
-            piece = keep.tile([P, PACK, count * P], F32, name="w_raw%d_%d" % (a, first))
+            piece = keep.tile([P, PACK, count * P], F32, name="w_raw", tag="w%d_%d" % (a, first))
             nc.sync.dma_start(piece[:], rows[:, :, first * P : (first + count) * P])
-            for m in range(first, first + count):
-                w_raw[a, m] = (piece, (m - first) * P)
+            w_raw[a, first] = piece
 
         def load_table(a):
-            table[a] = keep.tile([P, T], I32, name="table%d" % a)
+            table[a] = keep.tile([P, T], I32, name="table", tag="table%d" % a, align_bytes=64)
             nc.sync.dma_start(table[a][:], tab_words[a].rearrange("p t i -> p (t i)").bitcast(I32))
 
         load_weights(0, 0, 1)
         load_weights(0, 1, 1)
         load_weights(0, 2, 2)
+        for q in range(4):
+            nc.sync.dma_start(plane[32 * q : 32 * q + 4 * PASSES, :], tab_scales[:, 4 * q : 4 * q + 4, :].bitcast(I32))
         load_weights(1, 0, 4)
+        load_table(0)
+        load_weights(2, 0, 4)
+        load_table(1)
         bias = keep.tile([P, M // P], F32, name="bias")
         with nc.allow_non_contiguous_dma(reason="one bias value a partition"):
             nc.sync.dma_start(bias[:], b.rearrange("(c p) -> p c", p=P))
-        for a in range(PASSES):
-            for q in range(4):
-                row = 32 * q + 4 * a
-                nc.sync.dma_start(plane[row : row + 4, :], tab_scales[a, 4 * q : 4 * q + 4, :].bitcast(I32))
-        load_table(0)
-        load_table(1)
-        load_weights(2, 0, 4)
         load_table(2)
         for m in range(M // P):
             gates.append(keep.tile([P, T], F32, name="gates%d" % m))
@@ -74,8 +74,8 @@ def tile_list_tabgate_gelu_kernel(tc, tab_words, tab_scales, w, gT, b, offs, out
         picked_words = [keep.tile([P, S], U32, name="picked_words%d" % a, align_bytes=64) for a in range(PASSES)]
         weights = {}
 
-        def gather_scales(start, count):
-            nc.vector.tensor_copy(picked_scales[:, start : start + count], plane[:].bitcast(U8).indirect(picks(start, count)))
+        def gather_scales():
+            nc.vector.tensor_copy(picked_scales[:], plane[:].bitcast(U8).indirect(offsets[:]))
 
         def gather_words(a, start, count):
             nc.vector.tensor_copy(picked_words[a][:, start : start + count], table[a][:].bitcast(U32).indirect(picks(start, count)))
@@ -83,18 +83,32 @@ def tile_list_tabgate_gelu_kernel(tc, tab_words, tab_scales, w, gT, b, offs, out
         def grouped(ap):
             return ap.rearrange("p (c i t) -> p c t i", i=4, t=PACK)
 
-        def split_weights(a, first, count):
+        def split_weights(a, first, count, on_gpsimd):
             width = count * P
-            piece, col = w_raw[a, first]
-            blocks = slice(col // 4, (col + width) // 4)
+            piece = w_raw[a, first]
             upper = ring.tile([P, width * PACK], BF16, name="upper")
             halves = piece[:].bitcast(BF16).rearrange("p t (c i two) -> p c t i two", i=4, two=2)
-            nc.scalar.copy(grouped(upper[:]), halves[:, blocks, :, :, 1])
-            parts = ring.tile([P, 2, width * PACK], BF16, name="parts", align_bytes=64, bufs=3)
+            nc.scalar.copy(grouped(upper[:]), halves[:, :, :, :, 1])
+            if on_gpsimd:
+                parts = keep.tile([P, 2, width * PACK], BF16, name="parts", tag="lone", align_bytes=64)
+            else:
+                parts = ring.tile([P, 2, width * PACK], BF16, name="parts", tag="pair", align_bytes=64)
             nc.vector.tensor_scalar(parts[:, 0, :].bitcast(I32), upper[:].bitcast(I32), HI_MASK, None, ALU.bitwise_and)
-            whole = piece[:].rearrange("p t (c i) -> p c t i", i=4)
-            nc.vector.tensor_tensor(grouped(parts[:, 1, :]), whole[:, blocks, :, :], grouped(parts[:, 0, :]), ALU.subtract)
-            codes = keep.tile([P, 2, width], U32, name="codes%d_%d" % (a, first), align_bytes=64)
+            if on_gpsimd:
+                nc.gpsimd.tensor_tensor(
+                    parts[:, 1, :].rearrange("p (n t) -> p n t", t=PACK),
+                    piece[:].rearrange("p t n -> p n t"),
+                    parts[:, 0, :].rearrange("p (n t) -> p n t", t=PACK),
+                    ALU.subtract,
+                )
+            else:
+                whole = piece[:].rearrange("p t (c i) -> p c t i", i=4)
+                nc.vector.tensor_tensor(grouped(parts[:, 1, :]), whole, grouped(parts[:, 0, :]), ALU.subtract)
+            return parts
+
+        def quantise(parts, a, first, count, tag):
+            width = count * P
+            codes = keep.tile([P, 2, width], U32, name="codes", tag=tag, align_bytes=64)
             scales = keep.tile([P, 2, width], U8, name="scales%d_%d" % (a, first), align_bytes=64)
             nc.vector.quantize_mx(
                 codes[:].rearrange("p s n -> p (s n)").bitcast(FP8X4),
@@ -118,7 +132,16 @@ def tile_list_tabgate_gelu_kernel(tc, tab_words, tab_scales, w, gT, b, offs, out
                     stop=(a == PASSES - 1 and part == 1),
                 )
 
-        acts = {}
+        accs, acts, results = {}, {}, {}
+
+        def first_sums(a, step):
+            for start in range(0, S, step):
+                gather_words(a, start, step)
+                for s in range(start // BANK, (start + step) // BANK):
+                    for m in range(2):
+                        if a == 0:
+                            accs[m, s] = psum.tile([P, BANK], F32, name="acc")
+                        multiply(accs[m, s], a, m, s)
 
         def activate(acc, m, s):
             if s % 2 == 0:
@@ -128,40 +151,34 @@ def tile_list_tabgate_gelu_kernel(tc, tab_words, tab_scales, w, gT, b, offs, out
         def gate(m, start, count):
             act = acts[m, start // (2 * BANK)]
             lo = start % (2 * BANK)
-            result = ring.tile([P, count], F32, name="result", bufs=4)
-            nc.vector.tensor_tensor(result[:], gates[m][:].indirect(picks(start, count)), act[:, lo : lo + count], ALU.mult)
-            nc.sync.dma_start(out[P * m : P * (m + 1), start : start + count], result[:])
+            if start == 0:
+                results[m] = keep.tile([P, S], F32, name="result", tag=("w1_0", "w2_0", "result2", "result3")[m])
+            result = results[m][:, start : start + count]
+            nc.vector.tensor_tensor(result, gates[m][:].indirect(picks(start, count)), act[:, lo : lo + count], ALU.mult)
+            nc.sync.dma_start(out[P * m : P * (m + 1), start : start + count], result)
 
-        accs = {}
-        split_weights(0, 0, 1)
-        split_weights(0, 1, 1)
-        split_weights(0, 2, 2)
-        split_weights(1, 0, 2)
-        split_weights(1, 2, 2)
-        gather_scales(0, S)
+        for m in range(2):
+            quantise(split_weights(0, m, 1, False), 0, m, 1, "codes%d" % m)
+        parts = split_weights(0, 2, 2, True)
+        gather_scales()
+        quantise(parts, 0, 2, 2, "plane")
         for a in range(PASSES):
-            if a == PASSES - 1:
-                split_weights(a, 0, 2)
-            step = 1024 if a < PASSES - 1 else 512
-            for start in range(0, S, step):
-                gather_words(a, start, step)
-                for s in range(start // BANK, (start + step) // BANK):
-                    for m in range(2):
-                        if a == 0:
-                            accs[m, s] = psum.tile([P, BANK], F32, name="acc")
-                        multiply(accs[m, s], a, m, s)
-        split_weights(PASSES - 1, 2, 2)
-        for half in range(2):
-            for m in range(2):
-                for s in (2 * half, 2 * half + 1):
-                    activate(accs[m, s], m, s)
+            if a + 1 < PASSES:
+                parts = split_weights(a + 1, 0, 4, True)
+                first_sums(a, 1024)
+                quantise(parts, a + 1, 0, 4, "table%d" % a)
+            else:
+                first_sums(a, 512)
+        for m in range(2):
+            for s in range(S // BANK):
+                activate(accs[m, s], m, s)
         for m in range(2, 4):
             for s in range(S // BANK):
                 accs[m, s] = psum.tile([P, BANK], F32, name="acc")
                 for a in range(PASSES):
                     multiply(accs[m, s], a, m, s)
-        for start in range(0, S, 1024):
-            for m in range(2):
+        for m in range(2):
+            for start in range(0, S, 1024):
                 gate(m, start, 1024)
         for m in range(2, 4):
             for s in range(S // BANK):

@@ -1,6 +1,7 @@
 from contextlib import ExitStack
 
 import concourse.mybir as mybir
+from concourse.masks import make_identity
 
 K, M, T, S = 1536, 512, 4096, 2048
 FLOPS = 2 * 2 * K * M * S
@@ -19,6 +20,7 @@ P = 128
 PACK = 4
 PASSES = K // (P * PACK)
 BANK = 512
+UNITS = [[(0, 1, 2), (0, 3, 1)], [(1, 0, 2)], [(2, 0, 2), (1, 2, 1)], [(2, 2, 2), (1, 3, 1)]]
 HI_MASK = 0xFFF0FFF0 - (1 << 32)
 
 
@@ -40,6 +42,8 @@ def tile_list_tabgate_gelu_kernel(tc, tab_words, tab_scales, w, gT, b, offs, out
         warm = keep.tile([P, 2], F32, name="warm")
         nc.gpsimd.memset(warm[:, 0:1], 0.0)
         nc.scalar.activation(warm[:, 1:2], warm[:, 0:1], GELU)
+        identity = keep.tile([P, P], F32, name="identity")
+        make_identity(nc, identity[:])
 
         w_raw, table, gates = {}, {}, []
 
@@ -47,87 +51,102 @@ def tile_list_tabgate_gelu_kernel(tc, tab_words, tab_scales, w, gT, b, offs, out
             rows = w[512 * a : 512 * (a + 1), :].rearrange("(p t) n -> p t n", t=PACK)
             piece = keep.tile([P, PACK, count * P], F32, name="w_raw", tag="w%d_%d" % (a, first))
             nc.sync.dma_start(piece[:], rows[:, :, first * P : (first + count) * P])
-            w_raw[a, first] = piece
+            for m in range(first, first + count):
+                w_raw[a, m] = (piece, (m - first) * P)
 
         def load_table(a):
             table[a] = keep.tile([P, T], I32, name="table", tag="table%d" % a, align_bytes=64)
             nc.sync.dma_start(table[a][:], tab_words[a].rearrange("p t i -> p (t i)").bitcast(I32))
 
         load_weights(0, 0, 1)
-        load_weights(0, 1, 1)
-        load_weights(0, 2, 2)
+        load_weights(0, 1, 3)
         for q in range(4):
             nc.sync.dma_start(plane[32 * q : 32 * q + 4 * PASSES, :], tab_scales[:, 4 * q : 4 * q + 4, :].bitcast(I32))
-        load_weights(1, 0, 4)
+        bias_rows = keep.tile([P, P], F32, name="bias_rows")
+        nc.sync.dma_start(bias_rows[:], b.rearrange("(c p) -> c p", p=P).partition_broadcast(P // 4))
+        load_weights(1, 0, 2)
         load_table(0)
-        load_weights(2, 0, 4)
+        load_weights(2, 0, 2)
+        load_weights(1, 2, 2)
         load_table(1)
-        bias = keep.tile([P, M // P], F32, name="bias")
-        with nc.allow_non_contiguous_dma(reason="one bias value a partition"):
-            nc.sync.dma_start(bias[:], b.rearrange("(c p) -> p c", p=P))
+        load_weights(2, 2, 2)
         load_table(2)
         for m in range(M // P):
             gates.append(keep.tile([P, T], F32, name="gates%d" % m))
             nc.sync.dma_start(gates[m][:], gT[P * m : P * (m + 1), :])
 
-        picked_scales = keep.tile([P, S], U8, name="picked_scales", align_bytes=64)
-        picked_words = [keep.tile([P, S], U32, name="picked_words%d" % a, align_bytes=64) for a in range(PASSES)]
-        weights = {}
+        turned = psum.tile([P, P], F32, name="turned", tag="acc")
+        nc.tensor.transpose(turned[:], bias_rows[:], identity[:])
+        bias = keep.tile([P, M // P], F32, name="bias")
+        nc.scalar.copy(bias[:], turned[:, 0 : M // P])
+
+        picked, weights = {}, {}
 
         def gather_scales():
-            nc.vector.tensor_copy(picked_scales[:], plane[:].bitcast(U8).indirect(offsets[:]))
+            picked["scales"] = keep.tile([P, S], U8, name="picked_scales", tag="picked_scales", align_bytes=64)
+            nc.vector.tensor_copy(picked["scales"][:], plane[:].bitcast(U8).indirect(offsets[:]))
 
         def gather_words(a, start, count):
-            nc.vector.tensor_copy(picked_words[a][:, start : start + count], table[a][:].bitcast(U32).indirect(picks(start, count)))
+            if start == 0:
+                picked[a] = keep.tile([P, S], U32, name="picked_words", tag="picked%d" % a, align_bytes=64)
+            nc.vector.tensor_copy(picked[a][:, start : start + count], table[a][:].bitcast(U32).indirect(picks(start, count)))
 
         def grouped(ap):
             return ap.rearrange("p (c i t) -> p c t i", i=4, t=PACK)
 
-        def split_weights(a, first, count, on_gpsimd):
+        def split_weights(upper, a, first, count, parts, on_gpsimd):
             width = count * P
-            piece = w_raw[a, first]
-            upper = ring.tile([P, width * PACK], BF16, name="upper")
+            piece, col = w_raw[a, first]
+            blocks = slice(col // 4, (col + width) // 4)
             halves = piece[:].bitcast(BF16).rearrange("p t (c i two) -> p c t i two", i=4, two=2)
-            nc.scalar.copy(grouped(upper[:]), halves[:, :, :, :, 1])
-            if on_gpsimd:
-                parts = keep.tile([P, 2, width * PACK], BF16, name="parts", tag="lone", align_bytes=64)
-            else:
-                parts = ring.tile([P, 2, width * PACK], BF16, name="parts", tag="pair", align_bytes=64)
-            nc.vector.tensor_scalar(parts[:, 0, :].bitcast(I32), upper[:].bitcast(I32), HI_MASK, None, ALU.bitwise_and)
+            nc.scalar.copy(grouped(upper), halves[:, blocks, :, :, 1])
+            nc.vector.tensor_scalar(parts[:, 0, :].bitcast(I32), upper.bitcast(I32), HI_MASK, None, ALU.bitwise_and)
             if on_gpsimd:
                 nc.gpsimd.tensor_tensor(
                     parts[:, 1, :].rearrange("p (n t) -> p n t", t=PACK),
-                    piece[:].rearrange("p t n -> p n t"),
+                    piece[:].rearrange("p t n -> p n t")[:, col : col + width, :],
                     parts[:, 0, :].rearrange("p (n t) -> p n t", t=PACK),
                     ALU.subtract,
                 )
             else:
                 whole = piece[:].rearrange("p t (c i) -> p c t i", i=4)
-                nc.vector.tensor_tensor(grouped(parts[:, 1, :]), whole, grouped(parts[:, 0, :]), ALU.subtract)
-            return parts
+                nc.vector.tensor_tensor(grouped(parts[:, 1, :]), whole[:, blocks, :, :], grouped(parts[:, 0, :]), ALU.subtract)
 
-        def quantise(parts, a, first, count, tag):
+        def quantise(parts, codes, a, first, count):
             width = count * P
-            codes = keep.tile([P, 2, width], U32, name="codes", tag=tag, align_bytes=64)
-            scales = keep.tile([P, 2, width], U8, name="scales%d_%d" % (a, first), align_bytes=64)
-            nc.vector.quantize_mx(
-                codes[:].rearrange("p s n -> p (s n)").bitcast(FP8X4),
-                scales[:].rearrange("p s n -> p (s n)"),
-                parts[:].rearrange("p s x -> p (s x)"),
-            )
+            scales = keep.tile([P, 2 * width], U8, name="scales%d_%d" % (a, first), align_bytes=64)
+            nc.vector.quantize_mx(codes.bitcast(FP8X4), scales[:], parts[:].rearrange("p s x -> p (s x)"))
             for m in range(first, first + count):
-                weights[a, m] = (codes, scales, slice((m - first) * P, (m - first + 1) * P))
+                weights[a, m] = (codes, scales, width, (m - first) * P)
+
+        def split_on_gpsimd(units):
+            made = []
+            for a, first, count in units:
+                upper = ring.tile([P, count * P * PACK], BF16, name="upper", bufs=3)
+                parts = keep.tile([P, 2, count * P * PACK], BF16, name="parts", tag="parts%d" % count, align_bytes=64)
+                split_weights(upper[:], a, first, count, parts, True)
+                made.append(parts)
+            return made
+
+        def quantise_all(units, made, codes_tag):
+            total = sum(count for a, first, count in units)
+            codes = keep.tile([P, total * 2 * P], U32, name="codes", tag=codes_tag, align_bytes=64)
+            done = 0
+            for (a, first, count), parts in zip(units, made):
+                quantise(parts, codes[:, done * 2 * P : (done + count) * 2 * P], a, first, count)
+                done += count
 
         def multiply(acc, a, m, s):
-            codes, scales, wcols = weights[a, m]
+            codes, scales, width, col = weights[a, m]
             cols = slice(s * BANK, (s + 1) * BANK)
             for part in range(2):
+                wcols = slice(part * width + col, part * width + col + P)
                 nc.tensor.matmul_mx(
                     out=acc[:],
-                    lhsT=codes[:, part, wcols].bitcast(FP8X4),
-                    lhsT_scale=scales[:, part, wcols],
-                    rhs=picked_words[a][:, cols].bitcast(FP8X4),
-                    rhs_scale=picked_scales[4 * a :, cols],
+                    lhsT=codes[:, wcols].bitcast(FP8X4),
+                    lhsT_scale=scales[:, wcols],
+                    rhs=picked[a][:, cols].bitcast(FP8X4),
+                    rhs_scale=picked["scales"][4 * a :, cols],
                     start=(a == 0 and part == 0),
                     stop=(a == PASSES - 1 and part == 1),
                 )
@@ -152,23 +171,23 @@ def tile_list_tabgate_gelu_kernel(tc, tab_words, tab_scales, w, gT, b, offs, out
             act = acts[m, start // (2 * BANK)]
             lo = start % (2 * BANK)
             if start == 0:
-                results[m] = keep.tile([P, S], F32, name="result", tag=("w1_0", "w2_0", "result2", "result3")[m])
+                results[m] = keep.tile([P, S], F32, name="result", tag="result%d" % m)
             result = results[m][:, start : start + count]
             nc.vector.tensor_tensor(result, gates[m][:].indirect(picks(start, count)), act[:, lo : lo + count], ALU.mult)
             nc.sync.dma_start(out[P * m : P * (m + 1), start : start + count], result)
 
-        for m in range(2):
-            quantise(split_weights(0, m, 1, False), 0, m, 1, "codes%d" % m)
-        parts = split_weights(0, 2, 2, True)
+        upper = keep.tile([P, P * PACK], BF16, name="first_upper")
+        parts = keep.tile([P, 2, P * PACK], BF16, name="first_parts", tag="parts2", align_bytes=64)
+        codes = keep.tile([P, 2 * P], U32, name="first_codes", align_bytes=64)
+        split_weights(upper[:], 0, 0, 1, parts, False)
+        quantise(parts, codes[:], 0, 0, 1)
+        made = split_on_gpsimd(UNITS[0])
         gather_scales()
-        quantise(parts, 0, 2, 2, "plane")
+        quantise_all(UNITS[0], made, "plane")
         for a in range(PASSES):
-            if a + 1 < PASSES:
-                parts = split_weights(a + 1, 0, 4, True)
-                first_sums(a, 1024)
-                quantise(parts, a + 1, 0, 4, "table%d" % a)
-            else:
-                first_sums(a, 512)
+            made = split_on_gpsimd(UNITS[a + 1])
+            first_sums(a, 1024 if a + 1 < PASSES else 512)
+            quantise_all(UNITS[a + 1], made, "table%d" % a)
         for m in range(2):
             for s in range(S // BANK):
                 activate(accs[m, s], m, s)

@@ -19,9 +19,18 @@ GELU = mybir.ActivationFunctionType.Gelu_apprx_tanh
 P = 128
 PACK = 4
 PASSES = K // (P * PACK)
+TILES = M // P
 BANK = 512
-UNITS = [[(0, 1, 2), (0, 3, 1)], [(1, 0, 2)], [(2, 0, 2), (1, 2, 1)], [(2, 2, 2), (1, 3, 1)]]
+SLICES = S // BANK
 HI_MASK = 0xFFF0FFF0 - (1 << 32)
+BATCHES = [
+    [(0, 1, 2)],
+    [(1, 0, 2), (0, 3, 1)],
+    [(2, 0, 2), (1, 2, 1)],
+    [(2, 2, 2), (1, 3, 1)],
+]
+WORD_CUTS = [2048, 1024, 512]
+GATE_CUTS = [(1024, 1024), (2048,), (2048,), (1024, 512, 256, 256)]
 
 
 def tile_list_tabgate_gelu_kernel(tc, tab_words, tab_scales, w, gT, b, offs, out):
@@ -39,170 +48,156 @@ def tile_list_tabgate_gelu_kernel(tc, tab_words, tab_scales, w, gT, b, offs, out
 
         plane = keep.tile([P, T // 4], I32, name="plane", tag="plane", align_bytes=64)
         nc.vector.memset(plane[:], 0)
-        warm = keep.tile([P, 2], F32, name="warm")
-        nc.gpsimd.memset(warm[:, 0:1], 0.0)
-        nc.scalar.activation(warm[:, 1:2], warm[:, 0:1], GELU)
         identity = keep.tile([P, P], F32, name="identity")
-        make_identity(nc, identity[:])
+        nc.vector.memset(identity[:], 0.0)
+        make_identity(nc, identity[:], nomemset=True)
 
-        w_raw, table, gates = {}, {}, []
-
-        def load_weights(a, first, count):
-            rows = w[512 * a : 512 * (a + 1), :].rearrange("(p t) n -> p t n", t=PACK)
-            piece = keep.tile([P, PACK, count * P], F32, name="w_raw", tag="w%d_%d" % (a, first))
-            nc.sync.dma_start(piece[:], rows[:, :, first * P : (first + count) * P])
-            for m in range(first, first + count):
-                w_raw[a, m] = (piece, (m - first) * P)
+        def load_weights(name, runs):
+            raw = keep.tile([P, PACK, sum(count for a, first, count in runs) * P], F32, name=name)
+            col = 0
+            for a, first, count in runs:
+                rows = w[512 * a : 512 * (a + 1), :].rearrange("(p t) n -> p t n", t=PACK)
+                nc.sync.dma_start(raw[:, :, col : col + count * P], rows[:, :, first * P : (first + count) * P])
+                col += count * P
+            return raw
 
         def load_table(a):
-            table[a] = keep.tile([P, T], I32, name="table", tag="table%d" % a, align_bytes=64)
-            nc.sync.dma_start(table[a][:], tab_words[a].rearrange("p t i -> p (t i)").bitcast(I32))
+            table = keep.tile([P, T], I32, name="table", tag="table%d" % a, align_bytes=64)
+            nc.sync.dma_start(table[:], tab_words[a].rearrange("p t i -> p (t i)").bitcast(I32))
+            return table
 
-        load_weights(0, 0, 1)
-        load_weights(0, 1, 3)
+        first_raw = load_weights("first_raw", [(0, 0, 1)])
+        raws = [load_weights("raw0", BATCHES[0])]
         for q in range(4):
             nc.sync.dma_start(plane[32 * q : 32 * q + 4 * PASSES, :], tab_scales[:, 4 * q : 4 * q + 4, :].bitcast(I32))
         bias_rows = keep.tile([P, P], F32, name="bias_rows")
-        nc.sync.dma_start(bias_rows[:], b.rearrange("(c p) -> c p", p=P).partition_broadcast(P // 4))
-        load_weights(1, 0, 2)
-        load_table(0)
-        load_weights(2, 0, 2)
-        load_weights(1, 2, 2)
-        load_table(1)
-        load_weights(2, 2, 2)
-        load_table(2)
-        for m in range(M // P):
+        nc.sync.dma_start(bias_rows[:], b.rearrange("(c p) -> c p", p=P).partition_broadcast(P // TILES))
+        tables = []
+        for a in range(PASSES):
+            raws.append(load_weights("raw%d" % (a + 1), BATCHES[a + 1]))
+            tables.append(load_table(a))
+        gates = []
+        for m in range(TILES):
             gates.append(keep.tile([P, T], F32, name="gates%d" % m))
             nc.sync.dma_start(gates[m][:], gT[P * m : P * (m + 1), :])
 
         turned = psum.tile([P, P], F32, name="turned", tag="acc")
         nc.tensor.transpose(turned[:], bias_rows[:], identity[:])
-        bias = keep.tile([P, M // P], F32, name="bias")
-        nc.scalar.copy(bias[:], turned[:, 0 : M // P])
+        bias = keep.tile([P, TILES], F32, name="bias")
+        nc.scalar.copy(bias[:], turned[:, 0:TILES])
 
-        picked, weights = {}, {}
-
-        def gather_scales():
-            picked["scales"] = keep.tile([P, S], U8, name="picked_scales", tag="picked_scales", align_bytes=64)
-            nc.vector.tensor_copy(picked["scales"][:], plane[:].bitcast(U8).indirect(offsets[:]))
-
-        def gather_words(a, start, count):
-            if start == 0:
-                picked[a] = keep.tile([P, S], U32, name="picked_words", tag="picked%d" % a, align_bytes=64)
-            nc.vector.tensor_copy(picked[a][:, start : start + count], table[a][:].bitcast(U32).indirect(picks(start, count)))
+        picked_scales = keep.tile([P, S], U8, name="picked_scales", align_bytes=64)
+        picked_words = [keep.tile([P, S], U32, name="picked_words%d" % a, align_bytes=64) for a in range(PASSES)]
+        parts = keep.tile([P, 3, 2, P * PACK], BF16, name="parts", align_bytes=64)
+        weights = {}
 
         def grouped(ap):
             return ap.rearrange("p (c i t) -> p c t i", i=4, t=PACK)
 
-        def split_weights(upper, a, first, count, parts, on_gpsimd):
-            width = count * P
-            piece, col = w_raw[a, first]
-            blocks = slice(col // 4, (col + width) // 4)
-            halves = piece[:].bitcast(BF16).rearrange("p t (c i two) -> p c t i two", i=4, two=2)
-            nc.scalar.copy(grouped(upper), halves[:, blocks, :, :, 1])
-            nc.vector.tensor_scalar(parts[:, 0, :].bitcast(I32), upper.bitcast(I32), HI_MASK, None, ALU.bitwise_and)
-            if on_gpsimd:
-                nc.gpsimd.tensor_tensor(
-                    parts[:, 1, :].rearrange("p (n t) -> p n t", t=PACK),
-                    piece[:].rearrange("p t n -> p n t")[:, col : col + width, :],
-                    parts[:, 0, :].rearrange("p (n t) -> p n t", t=PACK),
-                    ALU.subtract,
-                )
-            else:
-                whole = piece[:].rearrange("p t (c i) -> p c t i", i=4)
-                nc.vector.tensor_tensor(grouped(parts[:, 1, :]), whole[:, blocks, :, :], grouped(parts[:, 0, :]), ALU.subtract)
+        def spans(blocks):
+            return [(0, min(blocks, 2))] + ([(2, 1)] if blocks == 3 else [])
 
-        def quantise(parts, codes, a, first, count):
-            width = count * P
-            scales = keep.tile([P, 2 * width], U8, name="scales%d_%d" % (a, first), align_bytes=64)
-            nc.vector.quantize_mx(codes.bitcast(FP8X4), scales[:], parts[:].rearrange("p s x -> p (s x)"))
-            for m in range(first, first + count):
-                weights[a, m] = (codes, scales, width, (m - first) * P)
-
-        def split_on_gpsimd(units):
-            made = []
-            for a, first, count in units:
+        def cut_hi(raw, blocks):
+            halves = raw[:].bitcast(BF16).rearrange("p t (c i two) -> p c t i two", i=4, two=2)
+            for first, count in spans(blocks):
                 upper = ring.tile([P, count * P * PACK], BF16, name="upper", bufs=3)
-                parts = keep.tile([P, 2, count * P * PACK], BF16, name="parts", tag="parts%d" % count, align_bytes=64)
-                split_weights(upper[:], a, first, count, parts, True)
-                made.append(parts)
-            return made
+                nc.scalar.copy(grouped(upper[:]), halves[:, first * P // 4 : (first + count) * P // 4, :, :, 1])
+                nc.vector.tensor_scalar(
+                    parts[:, first : first + count, 0, :].bitcast(I32),
+                    upper[:].bitcast(I32).rearrange("p (c x) -> p c x", c=count),
+                    HI_MASK,
+                    None,
+                    ALU.bitwise_and,
+                )
 
-        def quantise_all(units, made, codes_tag):
-            total = sum(count for a, first, count in units)
-            codes = keep.tile([P, total * 2 * P], U32, name="codes", tag=codes_tag, align_bytes=64)
-            done = 0
-            for (a, first, count), parts in zip(units, made):
-                quantise(parts, codes[:, done * 2 * P : (done + count) * 2 * P], a, first, count)
-                done += count
+        def split_on_gpsimd(raw, blocks):
+            cut_hi(raw, blocks)
+            nc.gpsimd.tensor_tensor(
+                parts[:, 0:blocks, 1, :].rearrange("p c (n t) -> p c n t", t=PACK),
+                raw[:].rearrange("p t (c n) -> p c n t", n=P),
+                parts[:, 0:blocks, 0, :].rearrange("p c (n t) -> p c n t", t=PACK),
+                ALU.subtract,
+            )
+
+        def quantise(runs, tag):
+            names = [(a, m) for a, first, count in runs for m in range(first, first + count)]
+            codes = keep.tile([P, len(names) * 2 * P], U32, name="codes", tag=tag, align_bytes=64)
+            scales = keep.tile([P, len(names) * 2 * P], U8, name="scales_" + tag, align_bytes=64)
+            for first, count in spans(len(names)):
+                cols = slice(first * 2 * P, (first + count) * 2 * P)
+                nc.vector.quantize_mx(
+                    codes[:, cols].bitcast(FP8X4),
+                    scales[:, cols],
+                    parts[:, first : first + count, :, :].rearrange("p c s x -> p (c s x)"),
+                )
+            for place, name in enumerate(names):
+                weights[name] = (codes, scales, place * 2 * P)
 
         def multiply(acc, a, m, s):
-            codes, scales, width, col = weights[a, m]
+            codes, scales, col = weights[a, m]
             cols = slice(s * BANK, (s + 1) * BANK)
             for part in range(2):
-                wcols = slice(part * width + col, part * width + col + P)
+                wcols = slice(col + part * P, col + (part + 1) * P)
                 nc.tensor.matmul_mx(
                     out=acc[:],
                     lhsT=codes[:, wcols].bitcast(FP8X4),
                     lhsT_scale=scales[:, wcols],
-                    rhs=picked[a][:, cols].bitcast(FP8X4),
-                    rhs_scale=picked["scales"][4 * a :, cols],
+                    rhs=picked_words[a][:, cols].bitcast(FP8X4),
+                    rhs_scale=picked_scales[4 * a :, cols],
                     start=(a == 0 and part == 0),
                     stop=(a == PASSES - 1 and part == 1),
                 )
 
-        accs, acts, results = {}, {}, {}
+        accs, acts = {}, {}
 
-        def first_sums(a, step):
+        def activate(m):
+            acts[m] = ring.tile([P, S], F32, name="act")
+            for s in range(SLICES):
+                nc.scalar.activation(acts[m][:, s * BANK : (s + 1) * BANK], accs[m, s][:], GELU, bias=bias[:, m : m + 1])
+
+        def gate(m):
+            result = keep.tile([P, S], F32, name="result%d" % m)
+            start = 0
+            for count in GATE_CUTS[m]:
+                cols = slice(start, start + count)
+                nc.vector.tensor_tensor(result[:, cols], gates[m][:].indirect(picks(start, count)), acts[m][:, cols], ALU.mult)
+                if m == TILES - 1:
+                    nc.sync.dma_start(out[P * m : P * (m + 1), cols], result[:, cols])
+                start += count
+            if m < TILES - 1:
+                nc.sync.dma_start(out[P * m : P * (m + 1), :], result[:])
+
+        cut_hi(first_raw, 1)
+        nc.vector.tensor_tensor(
+            grouped(parts[:, 0, 1, :]),
+            first_raw[:].rearrange("p t (c i) -> p c t i", i=4),
+            grouped(parts[:, 0, 0, :]),
+            ALU.subtract,
+        )
+        quantise([(0, 0, 1)], "first_codes")
+
+        split_on_gpsimd(raws[0], 2)
+        nc.vector.tensor_copy(picked_scales[:], plane[:].bitcast(U8).indirect(offsets[:]))
+        quantise(BATCHES[0], "plane")
+        for a in range(PASSES):
+            split_on_gpsimd(raws[a + 1], sum(count for pass_, first, count in BATCHES[a + 1]))
+            step = WORD_CUTS[a]
             for start in range(0, S, step):
-                gather_words(a, start, step)
+                nc.vector.tensor_copy(picked_words[a][:, start : start + step], tables[a][:].bitcast(U32).indirect(picks(start, step)))
                 for s in range(start // BANK, (start + step) // BANK):
                     for m in range(2):
                         if a == 0:
                             accs[m, s] = psum.tile([P, BANK], F32, name="acc")
                         multiply(accs[m, s], a, m, s)
-
-        def activate(acc, m, s):
-            if s % 2 == 0:
-                acts[m, s // 2] = ring.tile([P, 2 * BANK], F32, name="act", bufs=4)
-            nc.scalar.activation(acts[m, s // 2][:, (s % 2) * BANK : (s % 2 + 1) * BANK], acc[:], GELU, bias=bias[:, m : m + 1])
-
-        def gate(m, start, count):
-            act = acts[m, start // (2 * BANK)]
-            lo = start % (2 * BANK)
-            if start == 0:
-                results[m] = keep.tile([P, S], F32, name="result", tag="result%d" % m)
-            result = results[m][:, start : start + count]
-            nc.vector.tensor_tensor(result, gates[m][:].indirect(picks(start, count)), act[:, lo : lo + count], ALU.mult)
-            nc.sync.dma_start(out[P * m : P * (m + 1), start : start + count], result)
-
-        upper = keep.tile([P, P * PACK], BF16, name="first_upper")
-        parts = keep.tile([P, 2, P * PACK], BF16, name="first_parts", tag="parts2", align_bytes=64)
-        codes = keep.tile([P, 2 * P], U32, name="first_codes", align_bytes=64)
-        split_weights(upper[:], 0, 0, 1, parts, False)
-        quantise(parts, codes[:], 0, 0, 1)
-        made = split_on_gpsimd(UNITS[0])
-        gather_scales()
-        quantise_all(UNITS[0], made, "plane")
-        for a in range(PASSES):
-            made = split_on_gpsimd(UNITS[a + 1])
-            first_sums(a, 1024 if a + 1 < PASSES else 512)
-            quantise_all(UNITS[a + 1], made, "table%d" % a)
+            quantise(BATCHES[a + 1], "table%d" % a)
         for m in range(2):
-            for s in range(S // BANK):
-                activate(accs[m, s], m, s)
-        for m in range(2, 4):
-            for s in range(S // BANK):
+            activate(m)
+        for m in range(2, TILES):
+            for s in range(SLICES):
                 accs[m, s] = psum.tile([P, BANK], F32, name="acc")
                 for a in range(PASSES):
                     multiply(accs[m, s], a, m, s)
-        for m in range(2):
-            for start in range(0, S, 1024):
-                gate(m, start, 1024)
-        for m in range(2, 4):
-            for s in range(S // BANK):
-                activate(accs[m, s], m, s)
-            start = 0
-            for count in (1024, 1024) if m == 2 else (1024, 512, 256, 256):
-                gate(m, start, count)
-                start += count
+        for m in range(TILES):
+            if m >= 2:
+                activate(m)
+            gate(m)

@@ -24,10 +24,10 @@ BANK = 512
 SLICES = S // BANK
 HI_MASK = 0xFFF0FFF0 - (1 << 32)
 BATCHES = [
-    [(0, 1, 2)],
-    [(1, 0, 2), (0, 3, 1)],
-    [(2, 0, 2), (1, 2, 1)],
-    [(2, 2, 2), (1, 3, 1)],
+    [(0, 1), (0, 2), (0, 3)],
+    [(1, 0), (1, 1), (1, 2)],
+    [(2, 0), (2, 1), (2, 2)],
+    [(1, 3), (2, 3)],
 ]
 WORD_CUTS = [2048, 1024, 512]
 GATE_CUTS = [(1024, 1024), (2048,), (2048,), (1024, 512, 256, 256)]
@@ -52,30 +52,34 @@ def tile_list_tabgate_gelu_kernel(tc, tab_words, tab_scales, w, gT, b, offs, out
         nc.vector.memset(identity[:], 0.0)
         make_identity(nc, identity[:], nomemset=True)
 
-        def load_weights(name, runs):
-            raw = keep.tile([P, PACK, sum(count for a, first, count in runs) * P], F32, name=name)
-            col = 0
-            for a, first, count in runs:
-                rows = w[512 * a : 512 * (a + 1), :].rearrange("(p t) n -> p t n", t=PACK)
-                nc.sync.dma_start(raw[:, :, col : col + count * P], rows[:, :, first * P : (first + count) * P])
-                col += count * P
-            return raw
+        def weight_rows(a):
+            return w[512 * a : 512 * (a + 1), :].rearrange("(p t) n -> p t n", t=PACK)
 
         def load_table(a):
             table = keep.tile([P, T], I32, name="table", tag="table%d" % a, align_bytes=64)
             nc.sync.dma_start(table[:], tab_words[a].rearrange("p t i -> p (t i)").bitcast(I32))
             return table
 
-        first_raw = load_weights("first_raw", [(0, 0, 1)])
-        raws = [load_weights("raw0", BATCHES[0])]
+        w_first = keep.tile([P, PACK, P], F32, name="w_first")
+        nc.sync.dma_start(w_first[:], weight_rows(0)[:, :, 0:P])
+        w_rest = keep.tile([P, PACK, M - P], F32, name="w_rest")
+        nc.sync.dma_start(w_rest[:], weight_rows(0)[:, :, P:M])
         for q in range(4):
             nc.sync.dma_start(plane[32 * q : 32 * q + 4 * PASSES, :], tab_scales[:, 4 * q : 4 * q + 4, :].bitcast(I32))
         bias_rows = keep.tile([P, P], F32, name="bias_rows")
         nc.sync.dma_start(bias_rows[:], b.rearrange("(c p) -> c p", p=P).partition_broadcast(P // TILES))
+        w_later = keep.tile([P, PASSES - 1, PACK, M], F32, name="w_later")
         tables = []
         for a in range(PASSES):
-            raws.append(load_weights("raw%d" % (a + 1), BATCHES[a + 1]))
+            if a + 1 < PASSES:
+                nc.sync.dma_start(w_later[:, a, :, :], weight_rows(a + 1))
             tables.append(load_table(a))
+        sources = [
+            w_rest[:].rearrange("p t (c n) -> p c t n", n=P),
+            w_later[:, 0, :, 0 : M - P].rearrange("p t (c n) -> p c t n", n=P),
+            w_later[:, 1, :, 0 : M - P].rearrange("p t (c n) -> p c t n", n=P),
+            w_later[:, :, :, M - P : M],
+        ]
         gates = []
         for m in range(TILES):
             gates.append(keep.tile([P, T], F32, name="gates%d" % m))
@@ -92,35 +96,32 @@ def tile_list_tabgate_gelu_kernel(tc, tab_words, tab_scales, w, gT, b, offs, out
         weights = {}
 
         def grouped(ap):
-            return ap.rearrange("p (c i t) -> p c t i", i=4, t=PACK)
+            return ap.rearrange("p (g i t) -> p g t i", i=4, t=PACK)
 
         def spans(blocks):
             return [(0, min(blocks, 2))] + ([(2, 1)] if blocks == 3 else [])
 
-        def cut_hi(raw, blocks):
-            halves = raw[:].bitcast(BF16).rearrange("p t (c i two) -> p c t i two", i=4, two=2)
-            for first, count in spans(blocks):
-                upper = ring.tile([P, count * P * PACK], BF16, name="upper", bufs=3)
-                nc.scalar.copy(grouped(upper[:]), halves[:, first * P // 4 : (first + count) * P // 4, :, :, 1])
+        def cut_hi(source):
+            halves = source.bitcast(BF16).rearrange("p c t (g i two) -> p c g t i two", i=4, two=2)
+            for first, count in spans(source.shape[1]):
+                upper = ring.tile([P, count, P * PACK], BF16, name="upper", bufs=3)
+                for c in range(count):
+                    nc.scalar.copy(grouped(upper[:, c, :]), halves[:, first + c, :, :, :, 1])
                 nc.vector.tensor_scalar(
-                    parts[:, first : first + count, 0, :].bitcast(I32),
-                    upper[:].bitcast(I32).rearrange("p (c x) -> p c x", c=count),
-                    HI_MASK,
-                    None,
-                    ALU.bitwise_and,
+                    parts[:, first : first + count, 0, :].bitcast(I32), upper[:].bitcast(I32), HI_MASK, None, ALU.bitwise_and
                 )
 
-        def split_on_gpsimd(raw, blocks):
-            cut_hi(raw, blocks)
+        def split_on_gpsimd(source):
+            blocks = source.shape[1]
+            cut_hi(source)
             nc.gpsimd.tensor_tensor(
                 parts[:, 0:blocks, 1, :].rearrange("p c (n t) -> p c n t", t=PACK),
-                raw[:].rearrange("p t (c n) -> p c n t", n=P),
+                source.rearrange("p c t n -> p c n t"),
                 parts[:, 0:blocks, 0, :].rearrange("p c (n t) -> p c n t", t=PACK),
                 ALU.subtract,
             )
 
-        def quantise(runs, tag):
-            names = [(a, m) for a, first, count in runs for m in range(first, first + count)]
+        def quantise(names, tag):
             codes = keep.tile([P, len(names) * 2 * P], U32, name="codes", tag=tag, align_bytes=64)
             scales = keep.tile([P, len(names) * 2 * P], U8, name="scales_" + tag, align_bytes=64)
             for first, count in spans(len(names)):
@@ -167,20 +168,20 @@ def tile_list_tabgate_gelu_kernel(tc, tab_words, tab_scales, w, gT, b, offs, out
             if m < TILES - 1:
                 nc.sync.dma_start(out[P * m : P * (m + 1), :], result[:])
 
-        cut_hi(first_raw, 1)
+        cut_hi(w_first[:].rearrange("p t (c n) -> p c t n", n=P))
         nc.vector.tensor_tensor(
             grouped(parts[:, 0, 1, :]),
-            first_raw[:].rearrange("p t (c i) -> p c t i", i=4),
+            w_first[:].rearrange("p t (g i) -> p g t i", i=4),
             grouped(parts[:, 0, 0, :]),
             ALU.subtract,
         )
-        quantise([(0, 0, 1)], "first_codes")
+        quantise([(0, 0)], "first_codes")
 
-        split_on_gpsimd(raws[0], 2)
+        split_on_gpsimd(sources[0])
         nc.vector.tensor_copy(picked_scales[:], plane[:].bitcast(U8).indirect(offsets[:]))
         quantise(BATCHES[0], "plane")
         for a in range(PASSES):
-            split_on_gpsimd(raws[a + 1], sum(count for pass_, first, count in BATCHES[a + 1]))
+            split_on_gpsimd(sources[a + 1])
             step = WORD_CUTS[a]
             for start in range(0, S, step):
                 nc.vector.tensor_copy(picked_words[a][:, start : start + step], tables[a][:].bitcast(U32).indirect(picks(start, step)))

@@ -22,15 +22,13 @@ PASSES = K // (P * PACK)
 TILES = M // P
 BANK = 512
 SLICES = S // BANK
+BLOCK = P * PACK
 HI_MASK = 0xFFF0FFF0 - (1 << 32)
-BATCHES = [
-    [(0, 1), (0, 2), (0, 3)],
-    [(1, 0), (1, 1), (1, 2)],
-    [(2, 0), (2, 1), (2, 2)],
-    [(1, 3), (2, 3)],
-]
-WORD_CUTS = [2048, 1024, 512]
-GATE_CUTS = [(1024, 1024), (2048,), (2048,), (1024, 512, 256, 256)]
+SCALE_BASE = (0, 16, 64)
+HALF = 2 * BLOCK
+LEAD = 512
+PLANES_AT = 6 * HALF
+GATE_CUTS = [(1024, 1024), (2048,), (1024, 1024), (1024, 512, 256, 256)]
 
 
 def tile_list_tabgate_gelu_kernel(tc, tab_words, tab_scales, w, gT, b, offs, out):
@@ -38,6 +36,7 @@ def tile_list_tabgate_gelu_kernel(tc, tab_words, tab_scales, w, gT, b, offs, out
     with ExitStack() as ctx:
         keep = ctx.enter_context(tc.tile_pool(name="keep", bufs=1))
         ring = ctx.enter_context(tc.tile_pool(name="ring", bufs=2))
+        laid = ctx.enter_context(tc.tile_pool(name="laid", bufs=1))
         psum = ctx.enter_context(tc.psum_pool(name="psum", bufs=8))
 
         offsets = keep.tile([P, S // 16], U16, name="offsets")
@@ -46,118 +45,103 @@ def tile_list_tabgate_gelu_kernel(tc, tab_words, tab_scales, w, gT, b, offs, out
         def picks(start, count):
             return offsets[:, start // 16 : (start + count) // 16]
 
-        plane = keep.tile([P, T // 4], I32, name="plane", tag="plane", align_bytes=64)
-        nc.vector.memset(plane[:], 0)
-        identity = keep.tile([P, P], F32, name="identity")
-        nc.vector.memset(identity[:], 0.0)
-        make_identity(nc, identity[:], nomemset=True)
+        scale_rows = keep.tile([P, T // 4], I32, name="scale_rows", align_bytes=64)
+        nc.gpsimd.memset(scale_rows[64:128, :], 0)
+        nc.vector.memset(scale_rows[32:64, :], 0)
+        flat_scales = tab_scales.rearrange("a q t -> (a q) t").bitcast(I32)
+        nc.sync.dma_start(scale_rows[0:32, :], flat_scales[0:32, :])
+        raw = [keep.tile([P, PACK, M], F32, name="raw", tag="raw%d" % a) for a in range(PASSES)]
 
         def weight_rows(a):
             return w[512 * a : 512 * (a + 1), :].rearrange("(p t) n -> p t n", t=PACK)
 
-        def load_table(a):
-            table = keep.tile([P, T], I32, name="table", tag="table%d" % a, align_bytes=64)
-            nc.sync.dma_start(table[:], tab_words[a].rearrange("p t i -> p (t i)").bitcast(I32))
-            return table
+        tables = [keep.tile([P, T], I32, name="table", tag="table%d" % a, align_bytes=64) for a in range(PASSES)]
 
-        w_first = keep.tile([P, PACK, P], F32, name="w_first")
-        nc.sync.dma_start(w_first[:], weight_rows(0)[:, :, 0:P])
-        w_rest = keep.tile([P, PACK, M - P], F32, name="w_rest")
-        nc.sync.dma_start(w_rest[:], weight_rows(0)[:, :, P:M])
-        for q in range(4):
-            nc.sync.dma_start(plane[32 * q : 32 * q + 4 * PASSES, :], tab_scales[:, 4 * q : 4 * q + 4, :].bitcast(I32))
-        bias_rows = keep.tile([P, P], F32, name="bias_rows")
-        nc.sync.dma_start(bias_rows[:], b.rearrange("(c p) -> c p", p=P).partition_broadcast(P // TILES))
-        w_later = keep.tile([P, PASSES - 1, PACK, M], F32, name="w_later")
-        tables = []
-        for a in range(PASSES):
-            if a + 1 < PASSES:
-                nc.sync.dma_start(w_later[:, a, :, :], weight_rows(a + 1))
-            tables.append(load_table(a))
-        sources = [
-            w_rest[:].rearrange("p t (c n) -> p c t n", n=P),
-            w_later[:, 0, :, 0 : M - P].rearrange("p t (c n) -> p c t n", n=P),
-            w_later[:, 1, :, 0 : M - P].rearrange("p t (c n) -> p c t n", n=P),
-            w_later[:, :, :, M - P : M],
-        ]
+        def table_rows(a):
+            return tab_words[a].rearrange("p t i -> p (t i)").bitcast(I32)
+
+        nc.sync.dma_start(tables[0][:, 0:LEAD], table_rows(0)[:, 0:LEAD])
+        nc.sync.dma_start(scale_rows[64:80, :], flat_scales[32:48, :])
+
+        bias_rows = laid.tile([P, P], F32, name="bias_rows", offset=PLANES_AT + S - 256)
+        nc.gpsimd.memset(bias_rows[:], 0.0)
+        identity = laid.tile([P, P], F32, name="identity", offset=PLANES_AT + 2 * S + 256)
+        make_identity(nc, identity[:])
+
         gates = []
+        for a in range(PASSES):
+            nc.sync.dma_start(raw[a][:], weight_rows(a))
+            if a == 0:
+                nc.sync.dma_start(bias_rows[0:TILES, :], b.rearrange("(c p) -> c p", p=P))
+            first = LEAD if a == 0 else 0
+            nc.sync.dma_start(tables[a][:, first:T], table_rows(a)[:, first:T])
         for m in range(TILES):
-            gates.append(keep.tile([P, T], F32, name="gates%d" % m))
+            gates.append(keep.tile([P, T], F32, name="gates", tag="gates%d" % m))
             nc.sync.dma_start(gates[m][:], gT[P * m : P * (m + 1), :])
 
-        turned = psum.tile([P, P], F32, name="turned", tag="acc")
-        nc.tensor.transpose(turned[:], bias_rows[:], identity[:])
-        bias = keep.tile([P, TILES], F32, name="bias")
-        nc.scalar.copy(bias[:], turned[:, 0:TILES])
-
         picked_scales = keep.tile([P, S], U8, name="picked_scales", align_bytes=64)
-        picked_words = [keep.tile([P, S], U32, name="picked_words%d" % a, align_bytes=64) for a in range(PASSES)]
-        parts = keep.tile([P, 3, 2, P * PACK], BF16, name="parts", align_bytes=64)
-        weights = {}
+        picked, weights = {}, {}
 
         def grouped(ap):
             return ap.rearrange("p (g i t) -> p g t i", i=4, t=PACK)
 
-        def spans(blocks):
-            return [(0, min(blocks, 2))] + ([(2, 1)] if blocks == 3 else [])
+        def cut_hi(a):
+            upper = keep.tile([P, TILES * BLOCK], BF16, name="upper", tag="upper%d" % a, align_bytes=64)
+            halves = raw[a][:].bitcast(BF16).rearrange("p t (c g i two) -> p c g t i two", c=TILES, i=4, two=2)
+            for c in range(TILES):
+                nc.scalar.copy(grouped(upper[:, c * BLOCK : (c + 1) * BLOCK]), halves[:, c, :, :, :, 1])
+            hi = keep.tile([P, TILES * BLOCK], BF16, name="hi", tag="hi%d" % (a % 2), align_bytes=64)
+            nc.vector.tensor_scalar(hi[:].bitcast(I32), upper[:].bitcast(I32), HI_MASK, None, ALU.bitwise_and)
+            return hi
 
-        def cut_hi(source):
-            halves = source.bitcast(BF16).rearrange("p c t (g i two) -> p c g t i two", i=4, two=2)
-            for first, count in spans(source.shape[1]):
-                upper = ring.tile([P, count, P * PACK], BF16, name="upper", bufs=3)
-                for c in range(count):
-                    nc.scalar.copy(grouped(upper[:, c, :]), halves[:, first + c, :, :, :, 1])
-                nc.vector.tensor_scalar(
-                    parts[:, first : first + count, 0, :].bitcast(I32), upper[:].bitcast(I32), HI_MASK, None, ALU.bitwise_and
-                )
-
-        def split_on_gpsimd(source):
-            blocks = source.shape[1]
-            cut_hi(source)
-            nc.gpsimd.tensor_tensor(
-                parts[:, 0:blocks, 1, :].rearrange("p c (n t) -> p c n t", t=PACK),
-                source.rearrange("p c t n -> p c n t"),
-                parts[:, 0:blocks, 0, :].rearrange("p c (n t) -> p c n t", t=PACK),
-                ALU.subtract,
+        def cut_lo(a, half, hi, lo):
+            woven = keep.tile([P, HALF], F32, name="woven", tag="woven%d" % half)
+            nc.scalar.copy(
+                woven[:].rearrange("p (n t) -> p n t", t=PACK),
+                raw[a][:, :, half * 2 * P : (half + 1) * 2 * P].rearrange("p t n -> p n t"),
             )
+            nc.gpsimd.tensor_tensor(lo, woven[:], hi[:, half * HALF : (half + 1) * HALF], ALU.subtract)
 
-        def quantise(names, tag):
-            codes = keep.tile([P, len(names) * 2 * P], U32, name="codes", tag=tag, align_bytes=64)
-            scales = keep.tile([P, len(names) * 2 * P], U8, name="scales_" + tag, align_bytes=64)
-            for first, count in spans(len(names)):
-                cols = slice(first * 2 * P, (first + count) * 2 * P)
-                nc.vector.quantize_mx(
-                    codes[:, cols].bitcast(FP8X4),
-                    scales[:, cols],
-                    parts[:, first : first + count, :, :].rearrange("p c s x -> p (c s x)"),
-                )
-            for place, name in enumerate(names):
-                weights[name] = (codes, scales, place * 2 * P)
+        def quantise(tag, source, a, part, first):
+            count = source.shape[1] // BLOCK
+            codes = keep.tile([P, count * P], U32, name="codes", tag=tag, align_bytes=64)
+            scales = keep.tile([P, count * P], U8, name="scales_" + tag, align_bytes=64)
+            nc.vector.quantize_mx(codes[:].bitcast(FP8X4), scales[:], source[:])
+            for place in range(count):
+                weights[a, first + place, part] = (codes, scales, place * P)
 
-        def multiply(acc, a, m, s):
-            codes, scales, col = weights[a, m]
-            cols = slice(s * BANK, (s + 1) * BANK)
-            for part in range(2):
-                wcols = slice(col + part * P, col + (part + 1) * P)
-                nc.tensor.matmul_mx(
-                    out=acc[:],
-                    lhsT=codes[:, wcols].bitcast(FP8X4),
-                    lhsT_scale=scales[:, wcols],
-                    rhs=picked_words[a][:, cols].bitcast(FP8X4),
-                    rhs_scale=picked_scales[4 * a :, cols],
-                    start=(a == 0 and part == 0),
-                    stop=(a == PASSES - 1 and part == 1),
-                )
+        def gather_words(a, start, words):
+            count = words.shape[1]
+            nc.vector.tensor_copy(words[:], tables[a][:].bitcast(U32).indirect(picks(start, count)))
+            for s in range(count // BANK):
+                picked[a, start // BANK + s] = words[:, s * BANK : (s + 1) * BANK]
 
         accs, acts = {}, {}
 
-        def activate(m):
-            acts[m] = ring.tile([P, S], F32, name="act")
-            for s in range(SLICES):
-                nc.scalar.activation(acts[m][:, s * BANK : (s + 1) * BANK], accs[m, s][:], GELU, bias=bias[:, m : m + 1])
+        def multiply(a, part, m, s):
+            if (a, part) == (0, 0):
+                accs[m, s] = psum.tile([P, BANK], F32, name="acc")
+            codes, scales, col = weights[a, m, part]
+            nc.tensor.matmul_mx(
+                out=accs[m, s][:],
+                lhsT=codes[:, col : col + P].bitcast(FP8X4),
+                lhsT_scale=scales[:, col : col + P],
+                rhs=picked[a, s].bitcast(FP8X4),
+                rhs_scale=planes[a][:].bitcast(U8)[:, s * BANK : (s + 1) * BANK],
+                start=(a, part) == (0, 0),
+                stop=(a, part) == (PASSES - 1, 1),
+            )
+
+        def activate(m, s):
+            if s == 0:
+                acts[m] = ring.tile([P, S], F32, name="act")
+            nc.scalar.activation(acts[m][:, s * BANK : (s + 1) * BANK], accs[m, s][:], GELU, bias=bias[:, m : m + 1])
 
         def gate(m):
-            result = keep.tile([P, S], F32, name="result%d" % m)
+            if m < PASSES:
+                result = keep.tile([P, S], F32, name="result", tag="raw%d" % m)
+            else:
+                result = keep.tile([P, S], F32, name="result", tag="gates0")
             start = 0
             for count in GATE_CUTS[m]:
                 cols = slice(start, start + count)
@@ -168,37 +152,74 @@ def tile_list_tabgate_gelu_kernel(tc, tab_words, tab_scales, w, gT, b, offs, out
             if m < TILES - 1:
                 nc.sync.dma_start(out[P * m : P * (m + 1), :], result[:])
 
-        cut_hi(w_first[:].rearrange("p t (c n) -> p c t n", n=P))
-        nc.vector.tensor_tensor(
-            grouped(parts[:, 0, 1, :]),
-            w_first[:].rearrange("p t (g i) -> p g t i", i=4),
-            grouped(parts[:, 0, 0, :]),
-            ALU.subtract,
-        )
-        quantise([(0, 0)], "first_codes")
+        nc.vector.tensor_copy(picked_scales[:], scale_rows[:].bitcast(U8).indirect(offsets[:]))
 
-        split_on_gpsimd(sources[0])
-        nc.vector.tensor_copy(picked_scales[:], plane[:].bitcast(U8).indirect(offsets[:]))
-        quantise(BATCHES[0], "plane")
+        hi = cut_hi(0)
+        quantise("codes_hi0", hi, 0, 0, 0)
+
+        turned = psum.tile([P, P], F32, name="turned", tag="acc")
+        nc.tensor.transpose(turned[:], bias_rows[:], identity[:])
+        bias = keep.tile([P, TILES], F32, name="bias")
+        nc.scalar.copy(bias[:], turned[:, 0:TILES])
+        planes = []
         for a in range(PASSES):
-            split_on_gpsimd(sources[a + 1])
-            step = WORD_CUTS[a]
-            for start in range(0, S, step):
-                nc.vector.tensor_copy(picked_words[a][:, start : start + step], tables[a][:].bitcast(U32).indirect(picks(start, step)))
-                for s in range(start // BANK, (start + step) // BANK):
-                    for m in range(2):
-                        if a == 0:
-                            accs[m, s] = psum.tile([P, BANK], F32, name="acc")
-                        multiply(accs[m, s], a, m, s)
-            quantise(BATCHES[a + 1], "table%d" % a)
+            planes.append(laid.tile([P, S // 4], I32, name="plane%d" % a, offset=PLANES_AT + a * S, align_bytes=64))
+            nc.gpsimd.memset(planes[a][:], 0)
+
+        def lay_scales(a):
+            for i in range(4):
+                nc.scalar.dma_start(planes[a][i:P:32, :], picked_scales[:].bitcast(I32)[SCALE_BASE[a] + i : SCALE_BASE[a] + 16 : 4, :])
+
+        for a in range(PASSES - 1):
+            lo = laid.tile([P, TILES * BLOCK], BF16, name="lo%d" % a, offset=0, align_bytes=64)
+            for half in range(2):
+                cut_lo(a, half, hi, lo[:, half * HALF : (half + 1) * HALF])
+            if a == 1:
+                lay_scales(0)
+                lay_scales(1)
+            gather_words(a, 0, keep.tile([P, S], U32, name="words%d" % a, align_bytes=64))
+            hi = cut_hi(a + 1)
+            quantise("codes_hi%d" % (a + 1), hi, a + 1, 0, 0)
+            quantise("upper%d" % (a + 1), lo, a, 1, 0)
+
+        last = PASSES - 1
+        lo = laid.tile([P, HALF], BF16, name="lo_early", offset=HALF, align_bytes=64)
+        cut_lo(last, 0, hi, lo[:])
+        lay_scales(last)
+        gather_words(last, 0, keep.tile([P, S // 2], U32, name="words_early", align_bytes=64))
+        quantise("codes_early", lo, last, 1, 0)
+        lo = laid.tile([P, HALF], BF16, name="lo_late", offset=0, align_bytes=64)
+        cut_lo(last, 1, hi, lo[:])
+        gather_words(last, S // 2, laid.tile([P, S // 2], U32, name="words_late", offset=2 * HALF, align_bytes=64))
+        quantise("table%d" % last, lo, last, 1, 2)
+
+        for a in range(last):
+            for part in range(2):
+                for m in range(2):
+                    for s in range(SLICES):
+                        multiply(a, part, m, s)
+
+        def finish(m, s):
+            for part in range(2):
+                multiply(last, part, m, s)
+            activate(m, s)
+
+        def begin(m, s):
+            for a in range(last):
+                for part in range(2):
+                    multiply(a, part, m, s)
+
         for m in range(2):
-            activate(m)
-        for m in range(2, TILES):
-            for s in range(SLICES):
-                accs[m, s] = psum.tile([P, BANK], F32, name="acc")
-                for a in range(PASSES):
-                    multiply(accs[m, s], a, m, s)
+            for s in range(SLICES // 2):
+                finish(m, s)
+        begin(2, 0)
+        for m in range(2):
+            for s in range(SLICES // 2, SLICES):
+                finish(m, s)
         for m in range(TILES):
             if m >= 2:
-                activate(m)
+                for s in range(SLICES):
+                    if (m, s) != (2, 0):
+                        begin(m, s)
+                    finish(m, s)
             gate(m)

@@ -27,7 +27,6 @@ HI_MASK = 0xFFF0FFF0 - (1 << 32)
 SCALE_BASE = (0, 16, 64)
 HALF = 2 * BLOCK
 LEAD = 512
-PLANES_AT = 6 * HALF
 GATE_CUTS = [(1024, 1024), (2048,), (1024, 1024), (1024, 512, 256, 256)]
 
 
@@ -63,23 +62,37 @@ def tile_list_tabgate_gelu_kernel(tc, tab_words, tab_scales, w, gT, b, offs, out
         nc.sync.dma_start(tables[0][:, 0:LEAD], table_rows(0)[:, 0:LEAD])
         nc.sync.dma_start(scale_rows[64:80, :], flat_scales[32:48, :])
 
-        bias_rows = laid.tile([P, P], F32, name="bias_rows", offset=PLANES_AT + S - 256)
+        bias_rows = keep.tile([P, P], F32, name="bias_rows")
         nc.gpsimd.memset(bias_rows[:], 0.0)
-        identity = laid.tile([P, P], F32, name="identity", offset=PLANES_AT + 2 * S + 256)
+        identity = keep.tile([P, P], F32, name="identity")
         make_identity(nc, identity[:])
 
-        gates = []
+        picked_scales = keep.tile([P, S], U8, name="picked_scales", align_bytes=64)
+        nc.vector.tensor_copy(picked_scales[:], scale_rows[:].bitcast(U8).indirect(offsets[:]))
+        planes = []
         for a in range(PASSES):
-            nc.sync.dma_start(raw[a][:], weight_rows(a))
-            if a == 0:
-                nc.sync.dma_start(bias_rows[0:TILES, :], b.rearrange("(c p) -> c p", p=P))
-            first = LEAD if a == 0 else 0
-            nc.sync.dma_start(tables[a][:, first:T], table_rows(a)[:, first:T])
+            planes.append(keep.tile([P, S // 4], I32, name="plane%d" % a, align_bytes=64))
+            nc.gpsimd.memset(planes[a][:], 0)
+
+        def lay_scales(a):
+            for i in range(4):
+                nc.sync.dma_start(planes[a][i:P:32, :], picked_scales[:].bitcast(I32)[SCALE_BASE[a] + i : SCALE_BASE[a] + 16 : 4, :])
+
+        nc.sync.dma_start(raw[0][:], weight_rows(0))
+        nc.sync.dma_start(bias_rows[0:TILES, :], b.rearrange("(c p) -> c p", p=P))
+        nc.sync.dma_start(tables[0][:, LEAD:T], table_rows(0)[:, LEAD:T])
+        nc.sync.dma_start(raw[1][:], weight_rows(1))
+        lay_scales(0)
+        nc.sync.dma_start(tables[1][:], table_rows(1))
+        lay_scales(1)
+        nc.sync.dma_start(raw[2][:], weight_rows(2))
+        nc.sync.dma_start(tables[2][:], table_rows(2))
+        lay_scales(2)
+        gates = []
         for m in range(TILES):
             gates.append(keep.tile([P, T], F32, name="gates", tag="gates%d" % m))
             nc.sync.dma_start(gates[m][:], gT[P * m : P * (m + 1), :])
 
-        picked_scales = keep.tile([P, S], U8, name="picked_scales", align_bytes=64)
         picked, weights = {}, {}
 
         def grouped(ap):
@@ -152,8 +165,6 @@ def tile_list_tabgate_gelu_kernel(tc, tab_words, tab_scales, w, gT, b, offs, out
             if m < TILES - 1:
                 nc.sync.dma_start(out[P * m : P * (m + 1), :], result[:])
 
-        nc.vector.tensor_copy(picked_scales[:], scale_rows[:].bitcast(U8).indirect(offsets[:]))
-
         hi = cut_hi(0)
         quantise("codes_hi0", hi, 0, 0, 0)
 
@@ -161,22 +172,10 @@ def tile_list_tabgate_gelu_kernel(tc, tab_words, tab_scales, w, gT, b, offs, out
         nc.tensor.transpose(turned[:], bias_rows[:], identity[:])
         bias = keep.tile([P, TILES], F32, name="bias")
         nc.scalar.copy(bias[:], turned[:, 0:TILES])
-        planes = []
-        for a in range(PASSES):
-            planes.append(laid.tile([P, S // 4], I32, name="plane%d" % a, offset=PLANES_AT + a * S, align_bytes=64))
-            nc.gpsimd.memset(planes[a][:], 0)
-
-        def lay_scales(a):
-            for i in range(4):
-                nc.scalar.dma_start(planes[a][i:P:32, :], picked_scales[:].bitcast(I32)[SCALE_BASE[a] + i : SCALE_BASE[a] + 16 : 4, :])
-
         for a in range(PASSES - 1):
             lo = laid.tile([P, TILES * BLOCK], BF16, name="lo%d" % a, offset=0, align_bytes=64)
             for half in range(2):
                 cut_lo(a, half, hi, lo[:, half * HALF : (half + 1) * HALF])
-            if a == 1:
-                lay_scales(0)
-                lay_scales(1)
             gather_words(a, 0, keep.tile([P, S], U32, name="words%d" % a, align_bytes=64))
             hi = cut_hi(a + 1)
             quantise("codes_hi%d" % (a + 1), hi, a + 1, 0, 0)
@@ -185,7 +184,6 @@ def tile_list_tabgate_gelu_kernel(tc, tab_words, tab_scales, w, gT, b, offs, out
         last = PASSES - 1
         lo = laid.tile([P, HALF], BF16, name="lo_early", offset=HALF, align_bytes=64)
         cut_lo(last, 0, hi, lo[:])
-        lay_scales(last)
         gather_words(last, 0, keep.tile([P, S // 2], U32, name="words_early", align_bytes=64))
         quantise("codes_early", lo, last, 1, 0)
         lo = laid.tile([P, HALF], BF16, name="lo_late", offset=0, align_bytes=64)

@@ -24,9 +24,8 @@ BANK = 512
 SLICES = S // BANK
 BLOCK = P * PACK
 HI_MASK = 0xFFF0FFF0 - (1 << 32)
-SCALE_BASE = (0, 16, 64)
+SCALE_BASE = (32, 48, 112)
 HALF = 2 * BLOCK
-LEAD = 512
 GATE_CUTS = [(1024, 1024), (2048,), (1024, 1024), (1024, 512, 256, 256)]
 
 
@@ -35,7 +34,7 @@ def tile_list_tabgate_gelu_kernel(tc, tab_words, tab_scales, w, gT, b, offs, out
     with ExitStack() as ctx:
         keep = ctx.enter_context(tc.tile_pool(name="keep", bufs=1))
         ring = ctx.enter_context(tc.tile_pool(name="ring", bufs=2))
-        laid = ctx.enter_context(tc.tile_pool(name="laid", bufs=1))
+        early = ctx.enter_context(tc.tile_pool(name="early", bufs=1))
         psum = ctx.enter_context(tc.psum_pool(name="psum", bufs=8))
 
         offsets = keep.tile([P, S // 16], U16, name="offsets")
@@ -45,10 +44,11 @@ def tile_list_tabgate_gelu_kernel(tc, tab_words, tab_scales, w, gT, b, offs, out
             return offsets[:, start // 16 : (start + count) // 16]
 
         scale_rows = keep.tile([P, T // 4], I32, name="scale_rows", align_bytes=64)
-        nc.gpsimd.memset(scale_rows[64:128, :], 0)
-        nc.vector.memset(scale_rows[32:64, :], 0)
+        nc.vector.memset(scale_rows[0:32, :], 0)
+        nc.vector.memset(scale_rows[64:112, :], 0)
         flat_scales = tab_scales.rearrange("a q t -> (a q) t").bitcast(I32)
-        nc.sync.dma_start(scale_rows[0:32, :], flat_scales[0:32, :])
+        nc.sync.dma_start(scale_rows[32:64, :], flat_scales[0:32, :])
+        nc.sync.dma_start(scale_rows[112:128, :], flat_scales[32:48, :])
         raw = [keep.tile([P, PACK, M], F32, name="raw", tag="raw%d" % a) for a in range(PASSES)]
 
         def weight_rows(a):
@@ -59,19 +59,22 @@ def tile_list_tabgate_gelu_kernel(tc, tab_words, tab_scales, w, gT, b, offs, out
         def table_rows(a):
             return tab_words[a].rearrange("p t i -> p (t i)").bitcast(I32)
 
-        nc.sync.dma_start(tables[0][:, 0:LEAD], table_rows(0)[:, 0:LEAD])
-        nc.sync.dma_start(scale_rows[64:80, :], flat_scales[32:48, :])
-
-        bias_rows = keep.tile([P, P], F32, name="bias_rows")
-        nc.gpsimd.memset(bias_rows[:], 0.0)
-        identity = keep.tile([P, P], F32, name="identity")
+        bias_rows = early.tile([P, P], F32, name="bias_rows", offset=S - 256)
+        nc.gpsimd.memset(bias_rows[0 : P - TILES, :], 0.0)
+        nc.sync.dma_start(bias_rows[P - TILES : P, :], b.rearrange("(c p) -> c p", p=P))
+        identity = early.tile([P, P], F32, name="identity", offset=2 * S)
         make_identity(nc, identity[:])
+
+        turned = psum.tile([P, P], F32, name="turned", tag="acc")
+        nc.tensor.transpose(turned[:], bias_rows[:], identity[:])
+        bias = keep.tile([P, TILES], F32, name="bias")
+        nc.scalar.copy(bias[:], turned[:, P - TILES : P])
 
         picked_scales = keep.tile([P, S], U8, name="picked_scales", align_bytes=64)
         nc.vector.tensor_copy(picked_scales[:], scale_rows[:].bitcast(U8).indirect(offsets[:]))
         planes = []
         for a in range(PASSES):
-            planes.append(keep.tile([P, S // 4], I32, name="plane%d" % a, align_bytes=64))
+            planes.append(early.tile([P, S // 4], I32, name="plane%d" % a, offset=a * S, align_bytes=64))
             nc.gpsimd.memset(planes[a][:], 0)
 
         def lay_scales(a):
@@ -79,8 +82,7 @@ def tile_list_tabgate_gelu_kernel(tc, tab_words, tab_scales, w, gT, b, offs, out
                 nc.sync.dma_start(planes[a][i:P:32, :], picked_scales[:].bitcast(I32)[SCALE_BASE[a] + i : SCALE_BASE[a] + 16 : 4, :])
 
         nc.sync.dma_start(raw[0][:], weight_rows(0))
-        nc.sync.dma_start(bias_rows[0:TILES, :], b.rearrange("(c p) -> c p", p=P))
-        nc.sync.dma_start(tables[0][:, LEAD:T], table_rows(0)[:, LEAD:T])
+        nc.sync.dma_start(tables[0][:], table_rows(0))
         nc.sync.dma_start(raw[1][:], weight_rows(1))
         lay_scales(0)
         nc.sync.dma_start(tables[1][:], table_rows(1))
@@ -108,7 +110,7 @@ def tile_list_tabgate_gelu_kernel(tc, tab_words, tab_scales, w, gT, b, offs, out
             return hi
 
         def cut_lo(a, half, hi, lo):
-            woven = keep.tile([P, HALF], F32, name="woven", tag="woven%d" % half)
+            woven = keep.tile([P, HALF], F32, name="woven", tag="woven%d" % half, align_bytes=64)
             nc.scalar.copy(
                 woven[:].rearrange("p (n t) -> p n t", t=PACK),
                 raw[a][:, :, half * 2 * P : (half + 1) * 2 * P].rearrange("p t n -> p n t"),
@@ -168,12 +170,8 @@ def tile_list_tabgate_gelu_kernel(tc, tab_words, tab_scales, w, gT, b, offs, out
         hi = cut_hi(0)
         quantise("codes_hi0", hi, 0, 0, 0)
 
-        turned = psum.tile([P, P], F32, name="turned", tag="acc")
-        nc.tensor.transpose(turned[:], bias_rows[:], identity[:])
-        bias = keep.tile([P, TILES], F32, name="bias")
-        nc.scalar.copy(bias[:], turned[:, 0:TILES])
         for a in range(PASSES - 1):
-            lo = laid.tile([P, TILES * BLOCK], BF16, name="lo%d" % a, offset=0, align_bytes=64)
+            lo = hi
             for half in range(2):
                 cut_lo(a, half, hi, lo[:, half * HALF : (half + 1) * HALF])
             gather_words(a, 0, keep.tile([P, S], U32, name="words%d" % a, align_bytes=64))
@@ -182,13 +180,12 @@ def tile_list_tabgate_gelu_kernel(tc, tab_words, tab_scales, w, gT, b, offs, out
             quantise("upper%d" % (a + 1), lo, a, 1, 0)
 
         last = PASSES - 1
-        lo = laid.tile([P, HALF], BF16, name="lo_early", offset=HALF, align_bytes=64)
-        cut_lo(last, 0, hi, lo[:])
+        lo = lo[:, 0:HALF]
+        cut_lo(last, 0, hi, lo)
         gather_words(last, 0, keep.tile([P, S // 2], U32, name="words_early", align_bytes=64))
         quantise("codes_early", lo, last, 1, 0)
-        lo = laid.tile([P, HALF], BF16, name="lo_late", offset=0, align_bytes=64)
-        cut_lo(last, 1, hi, lo[:])
-        gather_words(last, S // 2, laid.tile([P, S // 2], U32, name="words_late", offset=2 * HALF, align_bytes=64))
+        cut_lo(last, 1, hi, lo)
+        gather_words(last, S // 2, keep.tile([P, S // 2], U32, name="words_late", tag="woven0", align_bytes=64))
         quantise("table%d" % last, lo, last, 1, 2)
 
         for a in range(last):

@@ -20,12 +20,14 @@ P = 128
 PACK = 4
 PASSES = K // (P * PACK)
 TILES = M // P
+OPEN = 2
 BANK = 512
 SLICES = S // BANK
 BLOCK = P * PACK
-HI_MASK = 0xFFF0FFF0 - (1 << 32)
-SCALE_BASE = (32, 48, 112)
 HALF = 2 * BLOCK
+HI_MASK = 0xFFF0FFF0 - (1 << 32)
+SCALE_ROWS = 16
+SCALE_BASE = (32, 48, 112)
 GATE_CUTS = [(1024, 1024), (2048,), (1024, 1024), (1024, 512, 256, 256)]
 
 
@@ -52,7 +54,7 @@ def tile_list_tabgate_gelu_kernel(tc, tab_words, tab_scales, w, gT, b, offs, out
         raw = [keep.tile([P, PACK, M], F32, name="raw", tag="raw%d" % a) for a in range(PASSES)]
 
         def weight_rows(a):
-            return w[512 * a : 512 * (a + 1), :].rearrange("(p t) n -> p t n", t=PACK)
+            return w[BLOCK * a : BLOCK * (a + 1), :].rearrange("(p t) n -> p t n", t=PACK)
 
         tables = [keep.tile([P, T], I32, name="table", tag="table%d" % a, align_bytes=64) for a in range(PASSES)]
 
@@ -78,8 +80,9 @@ def tile_list_tabgate_gelu_kernel(tc, tab_words, tab_scales, w, gT, b, offs, out
             nc.gpsimd.memset(planes[a][:], 0)
 
         def lay_scales(a):
+            base = SCALE_BASE[a]
             for i in range(4):
-                nc.sync.dma_start(planes[a][i:P:32, :], picked_scales[:].bitcast(I32)[SCALE_BASE[a] + i : SCALE_BASE[a] + 16 : 4, :])
+                nc.sync.dma_start(planes[a][i:P:32, :], picked_scales[:].bitcast(I32)[base + i : base + SCALE_ROWS : 4, :])
 
         nc.sync.dma_start(raw[0][:], weight_rows(0))
         nc.sync.dma_start(tables[0][:], table_rows(0))
@@ -105,7 +108,7 @@ def tile_list_tabgate_gelu_kernel(tc, tab_words, tab_scales, w, gT, b, offs, out
             halves = raw[a][:].bitcast(BF16).rearrange("p t (c g i two) -> p c g t i two", c=TILES, i=4, two=2)
             for c in range(TILES):
                 nc.scalar.copy(grouped(upper[:, c * BLOCK : (c + 1) * BLOCK]), halves[:, c, :, :, :, 1])
-            hi = keep.tile([P, TILES * BLOCK], BF16, name="hi", tag="hi%d" % (a % 2), align_bytes=64)
+            hi = keep.tile([P, TILES * BLOCK], BF16, name="hi", tag="hi%d" % min(a, 1), align_bytes=64)
             nc.vector.tensor_scalar(hi[:].bitcast(I32), upper[:].bitcast(I32), HI_MASK, None, ALU.bitwise_and)
             return hi
 
@@ -153,10 +156,7 @@ def tile_list_tabgate_gelu_kernel(tc, tab_words, tab_scales, w, gT, b, offs, out
             nc.scalar.activation(acts[m][:, s * BANK : (s + 1) * BANK], accs[m, s][:], GELU, bias=bias[:, m : m + 1])
 
         def gate(m):
-            if m < PASSES:
-                result = keep.tile([P, S], F32, name="result", tag="raw%d" % m)
-            else:
-                result = keep.tile([P, S], F32, name="result", tag="gates0")
+            result = keep.tile([P, S], F32, name="result", tag="raw%d" % m if m < PASSES else "gates0")
             start = 0
             for count in GATE_CUTS[m]:
                 cols = slice(start, start + count)
@@ -169,9 +169,9 @@ def tile_list_tabgate_gelu_kernel(tc, tab_words, tab_scales, w, gT, b, offs, out
 
         hi = cut_hi(0)
         quantise("codes_hi0", hi, 0, 0, 0)
-
-        for a in range(PASSES - 1):
-            lo = hi
+        lo = hi
+        last = PASSES - 1
+        for a in range(last):
             for half in range(2):
                 cut_lo(a, half, hi, lo[:, half * HALF : (half + 1) * HALF])
             gather_words(a, 0, keep.tile([P, S], U32, name="words%d" % a, align_bytes=64))
@@ -179,18 +179,16 @@ def tile_list_tabgate_gelu_kernel(tc, tab_words, tab_scales, w, gT, b, offs, out
             quantise("codes_hi%d" % (a + 1), hi, a + 1, 0, 0)
             quantise("upper%d" % (a + 1), lo, a, 1, 0)
 
-        last = PASSES - 1
-        lo = lo[:, 0:HALF]
-        cut_lo(last, 0, hi, lo)
+        cut_lo(last, 0, hi, lo[:, 0:HALF])
         gather_words(last, 0, keep.tile([P, S // 2], U32, name="words_early", align_bytes=64))
-        quantise("codes_early", lo, last, 1, 0)
-        cut_lo(last, 1, hi, lo)
+        quantise("codes_early", lo[:, 0:HALF], last, 1, 0)
+        cut_lo(last, 1, hi, lo[:, 0:HALF])
         gather_words(last, S // 2, keep.tile([P, S // 2], U32, name="words_late", tag="woven0", align_bytes=64))
-        quantise("table%d" % last, lo, last, 1, 2)
+        quantise("table%d" % last, lo[:, 0:HALF], last, 1, OPEN)
 
         for a in range(last):
             for part in range(2):
-                for m in range(2):
+                for m in range(OPEN):
                     for s in range(SLICES):
                         multiply(a, part, m, s)
 
@@ -204,17 +202,17 @@ def tile_list_tabgate_gelu_kernel(tc, tab_words, tab_scales, w, gT, b, offs, out
                 for part in range(2):
                     multiply(a, part, m, s)
 
-        for m in range(2):
+        for m in range(OPEN):
             for s in range(SLICES // 2):
                 finish(m, s)
-        begin(2, 0)
-        for m in range(2):
+        begin(OPEN, 0)
+        for m in range(OPEN):
             for s in range(SLICES // 2, SLICES):
                 finish(m, s)
         for m in range(TILES):
-            if m >= 2:
+            if m >= OPEN:
                 for s in range(SLICES):
-                    if (m, s) != (2, 0):
+                    if (m, s) != (OPEN, 0):
                         begin(m, s)
                     finish(m, s)
             gate(m)

@@ -37,6 +37,7 @@ def tile_list_tabgate_gelu_kernel(tc, tab_words, tab_scales, w, gT, b, offs, out
         keep = ctx.enter_context(tc.tile_pool(name="keep", bufs=1))
         ring = ctx.enter_context(tc.tile_pool(name="ring", bufs=2))
         early = ctx.enter_context(tc.tile_pool(name="early", bufs=1))
+        laid = ctx.enter_context(tc.tile_pool(name="laid", bufs=1))
         psum = ctx.enter_context(tc.psum_pool(name="psum", bufs=8))
 
         offsets = keep.tile([P, S // 16], U16, name="offsets")
@@ -72,7 +73,7 @@ def tile_list_tabgate_gelu_kernel(tc, tab_words, tab_scales, w, gT, b, offs, out
         bias = keep.tile([P, TILES], F32, name="bias")
         nc.scalar.copy(bias[:], turned[:, P - TILES : P])
 
-        picked_scales = keep.tile([P, S], U8, name="picked_scales", align_bytes=64)
+        picked_scales = keep.tile([P, S], U8, name="picked_scales", tag="picked_scales", align_bytes=64)
         nc.vector.tensor_copy(picked_scales[:], scale_rows[:].bitcast(U8).indirect(offsets[:]))
         planes = []
         for a in range(PASSES):
@@ -89,8 +90,8 @@ def tile_list_tabgate_gelu_kernel(tc, tab_words, tab_scales, w, gT, b, offs, out
         nc.sync.dma_start(raw[1][:], weight_rows(1))
         lay_scales(0)
         nc.sync.dma_start(tables[1][:], table_rows(1))
-        lay_scales(1)
         nc.sync.dma_start(raw[2][:], weight_rows(2))
+        lay_scales(1)
         nc.sync.dma_start(tables[2][:], table_rows(2))
         lay_scales(2)
         gates = []
@@ -108,7 +109,10 @@ def tile_list_tabgate_gelu_kernel(tc, tab_words, tab_scales, w, gT, b, offs, out
             halves = raw[a][:].bitcast(BF16).rearrange("p t (c g i two) -> p c g t i two", c=TILES, i=4, two=2)
             for c in range(TILES):
                 nc.scalar.copy(grouped(upper[:, c * BLOCK : (c + 1) * BLOCK]), halves[:, c, :, :, :, 1])
-            hi = keep.tile([P, TILES * BLOCK], BF16, name="hi", tag="hi%d" % min(a, 1), align_bytes=64)
+            if a == 0:
+                hi = laid.tile([P, TILES * BLOCK], BF16, name="hi_first", offset=0, align_bytes=64)
+            else:
+                hi = keep.tile([P, TILES * BLOCK], BF16, name="hi", align_bytes=64)
             nc.vector.tensor_scalar(hi[:].bitcast(I32), upper[:].bitcast(I32), HI_MASK, None, ALU.bitwise_and)
             return hi
 
@@ -179,12 +183,14 @@ def tile_list_tabgate_gelu_kernel(tc, tab_words, tab_scales, w, gT, b, offs, out
             quantise("codes_hi%d" % (a + 1), hi, a + 1, 0, 0)
             quantise("upper%d" % (a + 1), lo, a, 1, 0)
 
-        cut_lo(last, 0, hi, lo[:, 0:HALF])
+        lo = laid.tile([P, HALF], BF16, name="lo_early", offset=HALF, align_bytes=64)
+        cut_lo(last, 0, hi, lo[:])
         gather_words(last, 0, keep.tile([P, S // 2], U32, name="words_early", align_bytes=64))
-        quantise("codes_early", lo[:, 0:HALF], last, 1, 0)
-        cut_lo(last, 1, hi, lo[:, 0:HALF])
-        gather_words(last, S // 2, keep.tile([P, S // 2], U32, name="words_late", tag="woven0", align_bytes=64))
-        quantise("table%d" % last, lo[:, 0:HALF], last, 1, OPEN)
+        quantise("picked_scales", lo, last, 1, 0)
+        lo = laid.tile([P, HALF], BF16, name="lo_late", offset=0, align_bytes=64)
+        cut_lo(last, 1, hi, lo[:])
+        gather_words(last, S // 2, laid.tile([P, S // 2], U32, name="words_late", offset=2 * HALF, align_bytes=64))
+        quantise("table%d" % last, lo, last, 1, OPEN)
 
         for a in range(last):
             for part in range(2):
@@ -202,17 +208,13 @@ def tile_list_tabgate_gelu_kernel(tc, tab_words, tab_scales, w, gT, b, offs, out
                 for part in range(2):
                     multiply(a, part, m, s)
 
-        for m in range(OPEN):
-            for s in range(SLICES // 2):
-                finish(m, s)
-        begin(OPEN, 0)
-        for m in range(OPEN):
-            for s in range(SLICES // 2, SLICES):
-                finish(m, s)
+        for first in (0, SLICES // 2):
+            for m in range(OPEN):
+                for s in range(first, first + SLICES // 2):
+                    finish(m, s)
         for m in range(TILES):
             if m >= OPEN:
                 for s in range(SLICES):
-                    if (m, s) != (OPEN, 0):
-                        begin(m, s)
+                    begin(m, s)
                     finish(m, s)
             gate(m)

@@ -28,7 +28,7 @@ HALF = 2 * BLOCK
 HI_MASK = 0xFFF0FFF0 - (1 << 32)
 SCALE_ROWS = 16
 SCALE_BASE = (32, 48, 112)
-GATE_CUTS = [(1024, 1024), (2048,), (1024, 1024), (1024, 512, 256, 256)]
+GATE_CUTS = [(1024, 1024), (2048,), (1024, 1024), (1024, 768, 256)]
 
 
 def tile_list_tabgate_gelu_kernel(tc, tab_words, tab_scales, w, gT, b, offs, out):
@@ -106,13 +106,12 @@ def tile_list_tabgate_gelu_kernel(tc, tab_words, tab_scales, w, gT, b, offs, out
 
         def cut_hi(a):
             upper = keep.tile([P, TILES * BLOCK], BF16, name="upper", tag="upper%d" % a, align_bytes=64)
-            halves = raw[a][:].bitcast(BF16).rearrange("p t (c g i two) -> p c g t i two", c=TILES, i=4, two=2)
-            for c in range(TILES):
-                nc.scalar.copy(grouped(upper[:, c * BLOCK : (c + 1) * BLOCK]), halves[:, c, :, :, :, 1])
-            if a == 0:
-                hi = laid.tile([P, TILES * BLOCK], BF16, name="hi_first", offset=0, align_bytes=64)
+            halves = raw[a][:].bitcast(BF16).rearrange("p t (g i two) -> p g t i two", i=4, two=2)
+            nc.scalar.copy(grouped(upper[:]), halves[:, :, :, :, 1])
+            if a == 1:
+                hi = laid.tile([P, TILES * BLOCK], BF16, name="hi_middle", offset=0, align_bytes=64)
             else:
-                hi = keep.tile([P, TILES * BLOCK], BF16, name="hi", align_bytes=64)
+                hi = keep.tile([P, TILES * BLOCK], BF16, name="hi", tag="hi%d" % a, align_bytes=64)
             nc.vector.tensor_scalar(hi[:].bitcast(I32), upper[:].bitcast(I32), HI_MASK, None, ALU.bitwise_and)
             return hi
 
@@ -173,15 +172,15 @@ def tile_list_tabgate_gelu_kernel(tc, tab_words, tab_scales, w, gT, b, offs, out
 
         hi = cut_hi(0)
         quantise("codes_hi0", hi, 0, 0, 0)
-        lo = hi
         last = PASSES - 1
         for a in range(last):
+            lo = hi
             for half in range(2):
                 cut_lo(a, half, hi, lo[:, half * HALF : (half + 1) * HALF])
             gather_words(a, 0, keep.tile([P, S], U32, name="words%d" % a, align_bytes=64))
             hi = cut_hi(a + 1)
-            quantise("codes_hi%d" % (a + 1), hi, a + 1, 0, 0)
             quantise("upper%d" % (a + 1), lo, a, 1, 0)
+            quantise("hi%d" % a if a + 1 < last else "codes_hi%d" % last, hi, a + 1, 0, 0)
 
         lo = laid.tile([P, HALF], BF16, name="lo_early", offset=HALF, align_bytes=64)
         cut_lo(last, 0, hi, lo[:])

@@ -28,7 +28,7 @@ HALF = 2 * BLOCK
 HI_MASK = 0xFFF0FFF0 - (1 << 32)
 SCALE_ROWS = 16
 SCALE_BASE = (32, 48, 112)
-GATE_CUTS = [(1024, 1024), (2048,), (1024, 1024), (1024, 768, 256)]
+GATE_CUTS = [(1024, 1024), (2048,), (1024, 1024), (1024, 704, 320)]
 
 
 def tile_list_tabgate_gelu_kernel(tc, tab_words, tab_scales, w, gT, b, offs, out):
@@ -180,7 +180,7 @@ def tile_list_tabgate_gelu_kernel(tc, tab_words, tab_scales, w, gT, b, offs, out
             gather_words(a, 0, keep.tile([P, S], U32, name="words%d" % a, align_bytes=64))
             hi = cut_hi(a + 1)
             quantise("upper%d" % (a + 1), lo, a, 1, 0)
-            quantise("hi%d" % a if a + 1 < last else "codes_hi%d" % last, hi, a + 1, 0, 0)
+            quantise("codes_hi%d" % (a + 1), hi, a + 1, 0, 0)
 
         lo = laid.tile([P, HALF], BF16, name="lo_early", offset=HALF, align_bytes=64)
         cut_lo(last, 0, hi, lo[:])

@@ -108,10 +108,10 @@ def tile_list_tabgate_gelu_kernel(tc, tab_words, tab_scales, w, gT, b, offs, out
             upper = keep.tile([P, TILES * BLOCK], BF16, name="upper", tag="upper%d" % a, align_bytes=64)
             halves = raw[a][:].bitcast(BF16).rearrange("p t (g i two) -> p g t i two", i=4, two=2)
             nc.scalar.copy(grouped(upper[:]), halves[:, :, :, :, 1])
-            if a == 1:
-                hi = laid.tile([P, TILES * BLOCK], BF16, name="hi_middle", offset=0, align_bytes=64)
+            if a == 0:
+                hi = laid.tile([P, TILES * BLOCK], BF16, name="hi_first", offset=0, align_bytes=64)
             else:
-                hi = keep.tile([P, TILES * BLOCK], BF16, name="hi", tag="hi%d" % a, align_bytes=64)
+                hi = keep.tile([P, TILES * BLOCK], BF16, name="hi", align_bytes=64)
             nc.vector.tensor_scalar(hi[:].bitcast(I32), upper[:].bitcast(I32), HI_MASK, None, ALU.bitwise_and)
             return hi
 
@@ -172,9 +172,9 @@ def tile_list_tabgate_gelu_kernel(tc, tab_words, tab_scales, w, gT, b, offs, out
 
         hi = cut_hi(0)
         quantise("codes_hi0", hi, 0, 0, 0)
+        lo = hi
         last = PASSES - 1
         for a in range(last):
-            lo = hi
             for half in range(2):
                 cut_lo(a, half, hi, lo[:, half * HALF : (half + 1) * HALF])
             gather_words(a, 0, keep.tile([P, S], U32, name="words%d" % a, align_bytes=64))

@@ -28,7 +28,7 @@ HALF = 2 * BLOCK
 HI_MASK = 0xFFF0FFF0 - (1 << 32)
 SCALE_ROWS = 16
 SCALE_BASE = (32, 48, 112)
-GATE_CUTS = [(1024, 1024), (2048,), (1024, 1024), (1024, 704, 320)]
+GATE_CUTS = [(1024, 1024), (2048,), (1024, 1024), (1024, 512, 512)]
 
 
 def tile_list_tabgate_gelu_kernel(tc, tab_words, tab_scales, w, gT, b, offs, out):

@@ -80,20 +80,20 @@ def tile_list_tabgate_gelu_kernel(tc, tab_words, tab_scales, w, gT, b, offs, out
             planes.append(early.tile([P, S // 4], I32, name="plane%d" % a, offset=a * S, align_bytes=64))
             nc.gpsimd.memset(planes[a][:], 0)
 
-        def lay_scales(a):
-            base = SCALE_BASE[a]
-            for i in range(4):
-                nc.sync.dma_start(planes[a][i:P:32, :], picked_scales[:].bitcast(I32)[base + i : base + SCALE_ROWS : 4, :])
+        def lay_scales(moves):
+            for a, i in moves:
+                base = SCALE_BASE[a]
+                nc.sync.dma_start(planes[a][4 * a + i : P : 32, :], picked_scales[:].bitcast(I32)[base + i : base + SCALE_ROWS : 4, :])
 
         nc.sync.dma_start(raw[0][:], weight_rows(0))
         nc.sync.dma_start(tables[0][:], table_rows(0))
         nc.sync.dma_start(raw[1][:], weight_rows(1))
-        lay_scales(0)
+        lay_scales([(0, 0), (1, 0), (0, 1), (1, 1), (0, 2), (0, 3)])
         nc.sync.dma_start(tables[1][:], table_rows(1))
         nc.sync.dma_start(raw[2][:], weight_rows(2))
-        lay_scales(1)
+        lay_scales([(1, 2), (2, 0), (1, 3), (2, 1)])
         nc.sync.dma_start(tables[2][:], table_rows(2))
-        lay_scales(2)
+        lay_scales([(2, 2), (2, 3)])
         gates = []
         for m in range(TILES):
             gates.append(keep.tile([P, T], F32, name="gates", tag="gates%d" % m))
@@ -148,7 +148,7 @@ def tile_list_tabgate_gelu_kernel(tc, tab_words, tab_scales, w, gT, b, offs, out
                 lhsT=codes[:, col : col + P].bitcast(FP8X4),
                 lhsT_scale=scales[:, col : col + P],
                 rhs=picked[a, s].bitcast(FP8X4),
-                rhs_scale=planes[a][:].bitcast(U8)[:, s * BANK : (s + 1) * BANK],
+                rhs_scale=planes[a][:].bitcast(U8)[4 * a : P, s * BANK : (s + 1) * BANK],
                 start=(a, part) == (0, 0),
                 stop=(a, part) == (PASSES - 1, 1),
             )

@@ -28,7 +28,7 @@ HALF = 2 * BLOCK
 HI_MASK = 0xFFF0FFF0 - (1 << 32)
 SCALE_ROWS = 16
 SCALE_BASE = (32, 48, 112)
-GATE_CUTS = [(1024, 1024), (2048,), (1024, 1024), (1024, 512, 512)]
+GATE_CUTS = [(1024, 1024), (2048,), (2048,), (1024, 640, 256, 128)]
 
 
 def tile_list_tabgate_gelu_kernel(tc, tab_words, tab_scales, w, gT, b, offs, out):
@@ -91,9 +91,9 @@ def tile_list_tabgate_gelu_kernel(tc, tab_words, tab_scales, w, gT, b, offs, out
         lay_scales([(0, 0), (1, 0), (0, 1), (1, 1), (0, 2), (0, 3)])
         nc.sync.dma_start(tables[1][:], table_rows(1))
         nc.sync.dma_start(raw[2][:], weight_rows(2))
-        lay_scales([(1, 2), (2, 0), (1, 3), (2, 1)])
+        lay_scales([(2, 0), (1, 2), (2, 1), (1, 3), (2, 2)])
         nc.sync.dma_start(tables[2][:], table_rows(2))
-        lay_scales([(2, 2), (2, 3)])
+        lay_scales([(2, 3)])
         gates = []
         for m in range(TILES):
             gates.append(keep.tile([P, T], F32, name="gates", tag="gates%d" % m))
@@ -133,7 +133,7 @@ def tile_list_tabgate_gelu_kernel(tc, tab_words, tab_scales, w, gT, b, offs, out
 
         def gather_words(a, start, words):
             count = words.shape[1]
-            nc.vector.tensor_copy(words[:], tables[a][:].bitcast(U32).indirect(picks(start, count)))
+            nc.vector.tensor_copy(words[:, :], tables[a][:].bitcast(U32).indirect(picks(start, count)))
             for s in range(count // BANK):
                 picked[a, start // BANK + s] = words[:, s * BANK : (s + 1) * BANK]
 
@@ -159,7 +159,10 @@ def tile_list_tabgate_gelu_kernel(tc, tab_words, tab_scales, w, gT, b, offs, out
             nc.scalar.activation(acts[m][:, s * BANK : (s + 1) * BANK], accs[m, s][:], GELU, bias=bias[:, m : m + 1])
 
         def gate(m):
-            result = keep.tile([P, S], F32, name="result", tag="raw%d" % m if m < PASSES else "gates0")
+            if m < OPEN:
+                result = first_results[:, m, :]
+            else:
+                result = keep.tile([P, S], F32, name="result", tag="raw%d" % (m - OPEN))
             start = 0
             for count in GATE_CUTS[m]:
                 cols = slice(start, start + count)
@@ -167,7 +170,9 @@ def tile_list_tabgate_gelu_kernel(tc, tab_words, tab_scales, w, gT, b, offs, out
                 if m == TILES - 1:
                     nc.sync.dma_start(out[P * m : P * (m + 1), cols], result[:, cols])
                 start += count
-            if m < TILES - 1:
+            if m == OPEN - 1:
+                nc.sync.dma_start(out[0 : OPEN * P, :].rearrange("(m p) j -> p m j", p=P), first_results[:])
+            if m == OPEN:
                 nc.sync.dma_start(out[P * m : P * (m + 1), :], result[:])
 
         hi = cut_hi(0)
@@ -177,24 +182,29 @@ def tile_list_tabgate_gelu_kernel(tc, tab_words, tab_scales, w, gT, b, offs, out
         for a in range(last):
             for half in range(2):
                 cut_lo(a, half, hi, lo[:, half * HALF : (half + 1) * HALF])
-            gather_words(a, 0, keep.tile([P, S], U32, name="words%d" % a, align_bytes=64))
+            cut = S if a == 0 else S // 2
+            for start in range(0, S, cut):
+                gather_words(a, start, keep.tile([P, cut], U32, name="words%d_%d" % (a, start), align_bytes=64))
             hi = cut_hi(a + 1)
             quantise("upper%d" % (a + 1), lo, a, 1, 0)
             quantise("codes_hi%d" % (a + 1), hi, a + 1, 0, 0)
 
         lo = laid.tile([P, HALF], BF16, name="lo_early", offset=HALF, align_bytes=64)
         cut_lo(last, 0, hi, lo[:])
-        gather_words(last, 0, keep.tile([P, S // 2], U32, name="words_early", align_bytes=64))
+        for s in range(2):
+            gather_words(last, s * BANK, keep.tile([P, BANK], U32, name="words_early%d" % s, align_bytes=64))
         quantise("picked_scales", lo, last, 1, 0)
         lo = laid.tile([P, HALF], BF16, name="lo_late", offset=0, align_bytes=64)
         cut_lo(last, 1, hi, lo[:])
-        gather_words(last, S // 2, laid.tile([P, S // 2], U32, name="words_late", offset=2 * HALF, align_bytes=64))
+        late = laid.tile([P, S // 2], U32, name="words_late", offset=2 * HALF, align_bytes=64)
+        for s in range(2):
+            gather_words(last, (2 + s) * BANK, late[:, s * BANK : (s + 1) * BANK])
         quantise("table%d" % last, lo, last, 1, OPEN)
 
         for a in range(last):
             for part in range(2):
-                for m in range(OPEN):
-                    for s in range(SLICES):
+                for s in range(SLICES):
+                    for m in range(OPEN):
                         multiply(a, part, m, s)
 
         def finish(m, s):
@@ -207,10 +217,17 @@ def tile_list_tabgate_gelu_kernel(tc, tab_words, tab_scales, w, gT, b, offs, out
                 for part in range(2):
                     multiply(a, part, m, s)
 
-        for first in (0, SLICES // 2):
+        for s in range(SLICES // 2):
             for m in range(OPEN):
-                for s in range(first, first + SLICES // 2):
-                    finish(m, s)
+                multiply(last, 0, m, s)
+        for m in range(OPEN):
+            for s in range(SLICES // 2):
+                multiply(last, 1, m, s)
+                activate(m, s)
+        for s in range(SLICES // 2, SLICES):
+            for m in range(OPEN):
+                finish(m, s)
+        first_results = keep.tile([P, OPEN, S], F32, name="first_results", tag="table0", align_bytes=64)
         for m in range(TILES):
             if m >= OPEN:
                 for s in range(SLICES):

@@ -26,6 +26,7 @@ SLICES = S // BANK
 BLOCK = P * PACK
 HALF = 2 * BLOCK
 HI_MASK = 0xFFF0FFF0 - (1 << 32)
+LONG = 416
 SCALE_ROWS = 16
 SCALE_BASE = (32, 48, 112)
 GATE_CUTS = [(1024, 1024), (2048,), (2048,), (1024, 640, 256, 128)]
@@ -37,7 +38,7 @@ def tile_list_tabgate_gelu_kernel(tc, tab_words, tab_scales, w, gT, b, offs, out
         keep = ctx.enter_context(tc.tile_pool(name="keep", bufs=1))
         ring = ctx.enter_context(tc.tile_pool(name="ring", bufs=2))
         early = ctx.enter_context(tc.tile_pool(name="early", bufs=1))
-        laid = ctx.enter_context(tc.tile_pool(name="laid", bufs=1))
+        moved = ctx.enter_context(tc.tile_pool(name="moved", bufs=1))
         psum = ctx.enter_context(tc.psum_pool(name="psum", bufs=8))
 
         offsets = keep.tile([P, S // 16], U16, name="offsets")
@@ -73,7 +74,7 @@ def tile_list_tabgate_gelu_kernel(tc, tab_words, tab_scales, w, gT, b, offs, out
         bias = keep.tile([P, TILES], F32, name="bias")
         nc.scalar.copy(bias[:], turned[:, P - TILES : P])
 
-        picked_scales = keep.tile([P, S], U8, name="picked_scales", tag="picked_scales", align_bytes=64)
+        picked_scales = moved.tile([P, S], U8, name="picked_scales", offset=0, align_bytes=64)
         nc.vector.tensor_copy(picked_scales[:], scale_rows[:].bitcast(U8).indirect(offsets[:]))
         planes = []
         for a in range(PASSES):
@@ -91,9 +92,9 @@ def tile_list_tabgate_gelu_kernel(tc, tab_words, tab_scales, w, gT, b, offs, out
         lay_scales([(0, 0), (1, 0), (0, 1), (1, 1), (0, 2), (0, 3)])
         nc.sync.dma_start(tables[1][:], table_rows(1))
         nc.sync.dma_start(raw[2][:], weight_rows(2))
-        lay_scales([(2, 0), (1, 2), (2, 1), (1, 3), (2, 2)])
+        lay_scales([(1, 2), (2, 0), (1, 3)])
         nc.sync.dma_start(tables[2][:], table_rows(2))
-        lay_scales([(2, 3)])
+        lay_scales([(2, 1), (2, 2), (2, 3)])
         gates = []
         for m in range(TILES):
             gates.append(keep.tile([P, T], F32, name="gates", tag="gates%d" % m))
@@ -105,14 +106,12 @@ def tile_list_tabgate_gelu_kernel(tc, tab_words, tab_scales, w, gT, b, offs, out
             return ap.rearrange("p (g i t) -> p g t i", i=4, t=PACK)
 
         def cut_hi(a):
-            upper = keep.tile([P, TILES * BLOCK], BF16, name="upper", tag="upper%d" % a, align_bytes=64)
-            halves = raw[a][:].bitcast(BF16).rearrange("p t (g i two) -> p g t i two", i=4, two=2)
-            nc.scalar.copy(grouped(upper[:]), halves[:, :, :, :, 1])
-            if a == 0:
-                hi = laid.tile([P, TILES * BLOCK], BF16, name="hi_first", offset=0, align_bytes=64)
-            else:
-                hi = keep.tile([P, TILES * BLOCK], BF16, name="hi", align_bytes=64)
-            nc.vector.tensor_scalar(hi[:].bitcast(I32), upper[:].bitcast(I32), HI_MASK, None, ALU.bitwise_and)
+            hi = keep.tile([P, TILES * BLOCK], BF16, name="hi%d" % a, align_bytes=64)
+            for first, end in ([(0, M)] if a == 0 else [(0, LONG), (LONG, M)]):
+                upper = keep.tile([P, (end - first) * PACK], BF16, name="upper", tag="upper%d_%d" % (a, first), align_bytes=64)
+                halves = raw[a][:, :, first:end].bitcast(BF16).rearrange("p t (g i two) -> p g t i two", i=4, two=2)
+                nc.scalar.copy(grouped(upper[:]), halves[:, :, :, :, 1])
+                nc.vector.tensor_scalar(hi[:, first * PACK : end * PACK].bitcast(I32), upper[:].bitcast(I32), HI_MASK, None, ALU.bitwise_and)
             return hi
 
         def cut_lo(a, half, hi, lo):
@@ -123,11 +122,14 @@ def tile_list_tabgate_gelu_kernel(tc, tab_words, tab_scales, w, gT, b, offs, out
             )
             nc.gpsimd.tensor_tensor(lo, woven[:], hi[:, half * HALF : (half + 1) * HALF], ALU.subtract)
 
-        def quantise(tag, source, a, part, first):
+        def quantise(tag, source, a, part, first, pool=keep, offset=None):
             count = source.shape[1] // BLOCK
-            codes = keep.tile([P, count * P], U32, name="codes", tag=tag, align_bytes=64)
+            if offset is None:
+                codes = keep.tile([P, count * P], U32, name="codes", tag=tag, align_bytes=64)
+            else:
+                codes = moved.tile([P, count * P], U32, name=tag, offset=offset, align_bytes=64)
             scales = keep.tile([P, count * P], U8, name="scales_" + tag, align_bytes=64)
-            nc.vector.quantize_mx(codes[:].bitcast(FP8X4), scales[:], source[:])
+            nc.vector.quantize_mx(codes[:].bitcast(FP8X4), scales[:], source[:, :])
             for place in range(count):
                 weights[a, first + place, part] = (codes, scales, place * P)
 
@@ -186,20 +188,19 @@ def tile_list_tabgate_gelu_kernel(tc, tab_words, tab_scales, w, gT, b, offs, out
             for start in range(0, S, cut):
                 gather_words(a, start, keep.tile([P, cut], U32, name="words%d_%d" % (a, start), align_bytes=64))
             hi = cut_hi(a + 1)
-            quantise("upper%d" % (a + 1), lo, a, 1, 0)
+            quantise("upper%d_0" % (a + 1), lo, a, 1, 0)
             quantise("codes_hi%d" % (a + 1), hi, a + 1, 0, 0)
 
-        lo = laid.tile([P, HALF], BF16, name="lo_early", offset=HALF, align_bytes=64)
-        cut_lo(last, 0, hi, lo[:])
+        lo = lo[:, 0:HALF]
+        cut_lo(last, 0, hi, lo)
         for s in range(2):
             gather_words(last, s * BANK, keep.tile([P, BANK], U32, name="words_early%d" % s, align_bytes=64))
-        quantise("picked_scales", lo, last, 1, 0)
-        lo = laid.tile([P, HALF], BF16, name="lo_late", offset=0, align_bytes=64)
-        cut_lo(last, 1, hi, lo[:])
-        late = laid.tile([P, S // 2], U32, name="words_late", offset=2 * HALF, align_bytes=64)
+        quantise("codes_lo_early", lo, last, 1, 0, offset=0)
+        cut_lo(last, 1, hi, lo)
+        late = moved.tile([P, S // 2], U32, name="words_late", offset=S // 2, align_bytes=64)
         for s in range(2):
             gather_words(last, (2 + s) * BANK, late[:, s * BANK : (s + 1) * BANK])
-        quantise("table%d" % last, lo, last, 1, OPEN)
+        quantise("codes_lo_late", lo, last, 1, OPEN)
 
         for a in range(last):
             for part in range(2):

@@ -107,7 +107,7 @@ def tile_list_tabgate_gelu_kernel(tc, tab_words, tab_scales, w, gT, b, offs, out
 
         def cut_hi(a):
             hi = keep.tile([P, TILES * BLOCK], BF16, name="hi%d" % a, align_bytes=64)
-            for first, end in ([(0, M)] if a == 0 else [(0, LONG), (LONG, M)]):
+            for first, end in ([(M - LONG, M), (0, M - LONG)] if a == 0 else [(0, LONG), (LONG, M)]):
                 upper = keep.tile([P, (end - first) * PACK], BF16, name="upper", tag="upper%d_%d" % (a, first), align_bytes=64)
                 halves = raw[a][:, :, first:end].bitcast(BF16).rearrange("p t (g i two) -> p g t i two", i=4, two=2)
                 nc.scalar.copy(grouped(upper[:]), halves[:, :, :, :, 1])
@@ -178,7 +178,8 @@ def tile_list_tabgate_gelu_kernel(tc, tab_words, tab_scales, w, gT, b, offs, out
                 nc.sync.dma_start(out[P * m : P * (m + 1), :], result[:])
 
         hi = cut_hi(0)
-        quantise("codes_hi0", hi, 0, 0, 0)
+        quantise("codes_hi0_rest", hi[:, BLOCK : TILES * BLOCK], 0, 0, 1)
+        quantise("codes_hi0_first", hi[:, 0:BLOCK], 0, 0, 0)
         lo = hi
         last = PASSES - 1
         for a in range(last):
@@ -191,11 +192,12 @@ def tile_list_tabgate_gelu_kernel(tc, tab_words, tab_scales, w, gT, b, offs, out
             quantise("upper%d_0" % (a + 1), lo, a, 1, 0)
             quantise("codes_hi%d" % (a + 1), hi, a + 1, 0, 0)
 
-        lo = lo[:, 0:HALF]
-        cut_lo(last, 0, hi, lo)
-        for s in range(2):
-            gather_words(last, s * BANK, keep.tile([P, BANK], U32, name="words_early%d" % s, align_bytes=64))
-        quantise("codes_lo_early", lo, last, 1, 0, offset=0)
+        spare = lo
+        cut_lo(last, 0, hi, spare[:, BLOCK : BLOCK + HALF])
+        gather_words(last, 0, keep.tile([P, S // 2], U32, name="words_early", align_bytes=64))
+        for m in range(OPEN):
+            quantise("codes_lo_early%d" % m, spare[:, (m + 1) * BLOCK : (m + 2) * BLOCK], last, 1, m, offset=m * P * PACK)
+        lo = spare[:, 0:HALF]
         cut_lo(last, 1, hi, lo)
         late = moved.tile([P, S // 2], U32, name="words_late", offset=S // 2, align_bytes=64)
         for s in range(2):
@@ -218,13 +220,9 @@ def tile_list_tabgate_gelu_kernel(tc, tab_words, tab_scales, w, gT, b, offs, out
                 for part in range(2):
                     multiply(a, part, m, s)
 
-        for s in range(SLICES // 2):
-            for m in range(OPEN):
-                multiply(last, 0, m, s)
         for m in range(OPEN):
             for s in range(SLICES // 2):
-                multiply(last, 1, m, s)
-                activate(m, s)
+                finish(m, s)
         for s in range(SLICES // 2, SLICES):
             for m in range(OPEN):
                 finish(m, s)

@@ -107,7 +107,7 @@ def tile_list_tabgate_gelu_kernel(tc, tab_words, tab_scales, w, gT, b, offs, out
 
         def cut_hi(a):
             hi = keep.tile([P, TILES * BLOCK], BF16, name="hi%d" % a, align_bytes=64)
-            for first, end in ([(M - LONG, M), (0, M - LONG)] if a == 0 else [(0, LONG), (LONG, M)]):
+            for first, end in ([(0, M)] if a == 0 else [(0, LONG), (LONG, M)]):
                 upper = keep.tile([P, (end - first) * PACK], BF16, name="upper", tag="upper%d_%d" % (a, first), align_bytes=64)
                 halves = raw[a][:, :, first:end].bitcast(BF16).rearrange("p t (g i two) -> p g t i two", i=4, two=2)
                 nc.scalar.copy(grouped(upper[:]), halves[:, :, :, :, 1])
@@ -178,8 +178,7 @@ def tile_list_tabgate_gelu_kernel(tc, tab_words, tab_scales, w, gT, b, offs, out
                 nc.sync.dma_start(out[P * m : P * (m + 1), :], result[:])
 
         hi = cut_hi(0)
-        quantise("codes_hi0_rest", hi[:, BLOCK : TILES * BLOCK], 0, 0, 1)
-        quantise("codes_hi0_first", hi[:, 0:BLOCK], 0, 0, 0)
+        quantise("codes_hi0", hi, 0, 0, 0)
         lo = hi
         last = PASSES - 1
         for a in range(last):

@@ -49,7 +49,7 @@ def tile_list_tabgate_gelu_kernel(tc, tab_words, tab_scales, w, gT, b, offs, out
 
         scale_rows = keep.tile([P, T // 4], I32, name="scale_rows", align_bytes=64)
         nc.vector.memset(scale_rows[0:32, :], 0)
-        nc.vector.memset(scale_rows[64:112, :], 0)
+        nc.gpsimd.memset(scale_rows[64:112, :], 0)
         flat_scales = tab_scales.rearrange("a q t -> (a q) t").bitcast(I32)
         nc.sync.dma_start(scale_rows[32:64, :], flat_scales[0:32, :])
         nc.sync.dma_start(scale_rows[112:128, :], flat_scales[32:48, :])

@@ -37,7 +37,6 @@ def tile_list_tabgate_gelu_kernel(tc, tab_words, tab_scales, w, gT, b, offs, out
     with ExitStack() as ctx:
         keep = ctx.enter_context(tc.tile_pool(name="keep", bufs=1))
         ring = ctx.enter_context(tc.tile_pool(name="ring", bufs=2))
-        early = ctx.enter_context(tc.tile_pool(name="early", bufs=1))
         moved = ctx.enter_context(tc.tile_pool(name="moved", bufs=1))
         psum = ctx.enter_context(tc.psum_pool(name="psum", bufs=8))
 
@@ -63,23 +62,18 @@ def tile_list_tabgate_gelu_kernel(tc, tab_words, tab_scales, w, gT, b, offs, out
         def table_rows(a):
             return tab_words[a].rearrange("p t i -> p (t i)").bitcast(I32)
 
-        bias_rows = early.tile([P, P], F32, name="bias_rows", offset=S - 256)
-        nc.gpsimd.memset(bias_rows[0 : P - TILES, :], 0.0)
-        nc.sync.dma_start(bias_rows[P - TILES : P, :], b.rearrange("(c p) -> c p", p=P))
-        identity = early.tile([P, P], F32, name="identity", offset=2 * S)
-        make_identity(nc, identity[:])
+        planes = []
+        for a in range(PASSES):
+            planes.append(keep.tile([P, S // 4], I32, name="plane%d" % a, align_bytes=64))
+            nc.gpsimd.memset(planes[a][:], 0)
 
-        turned = psum.tile([P, P], F32, name="turned", tag="acc")
-        nc.tensor.transpose(turned[:], bias_rows[:], identity[:])
-        bias = keep.tile([P, TILES], F32, name="bias")
-        nc.scalar.copy(bias[:], turned[:, P - TILES : P])
+        bias_rows = keep.tile([P, P], F32, name="bias_rows")
+        nc.gpsimd.memset(bias_rows[0 : P - TILES, :], 0.0)
+        identity = keep.tile([P, P], F32, name="identity")
+        make_identity(nc, identity[:])
 
         picked_scales = moved.tile([P, S], U8, name="picked_scales", offset=0, align_bytes=64)
         nc.vector.tensor_copy(picked_scales[:], scale_rows[:].bitcast(U8).indirect(offsets[:]))
-        planes = []
-        for a in range(PASSES):
-            planes.append(early.tile([P, S // 4], I32, name="plane%d" % a, offset=a * S, align_bytes=64))
-            nc.gpsimd.memset(planes[a][:], 0)
 
         def lay_scales(moves):
             for a, i in moves:
@@ -88,6 +82,11 @@ def tile_list_tabgate_gelu_kernel(tc, tab_words, tab_scales, w, gT, b, offs, out
 
         nc.sync.dma_start(raw[0][:], weight_rows(0))
         nc.sync.dma_start(tables[0][:], table_rows(0))
+        nc.sync.dma_start(bias_rows[P - TILES : P, :], b.rearrange("(c p) -> c p", p=P))
+        turned = psum.tile([P, P], F32, name="turned", tag="acc")
+        nc.tensor.transpose(turned[:], bias_rows[:], identity[:])
+        bias = keep.tile([P, TILES], F32, name="bias")
+        nc.scalar.copy(bias[:], turned[:, P - TILES : P])
         nc.sync.dma_start(raw[1][:], weight_rows(1))
         lay_scales([(0, 0), (1, 0), (0, 1), (1, 1), (0, 2), (0, 3)])
         nc.sync.dma_start(tables[1][:], table_rows(1))

@@ -108,8 +108,13 @@ def tile_list_tabgate_gelu_kernel(tc, tab_words, tab_scales, w, gT, b, offs, out
             hi = keep.tile([P, TILES * BLOCK], BF16, name="hi%d" % a, align_bytes=64)
             for first, end in ([(0, M)] if a == 0 else [(0, LONG), (LONG, M)]):
                 upper = keep.tile([P, (end - first) * PACK], BF16, name="upper", tag="upper%d_%d" % (a, first), align_bytes=64)
-                halves = raw[a][:, :, first:end].bitcast(BF16).rearrange("p t (g i two) -> p g t i two", i=4, two=2)
-                nc.scalar.copy(grouped(upper[:]), halves[:, :, :, :, 1])
+                shared = M // 2 if a == 0 else 0
+                if shared:
+                    pairs = raw[a][:, :, 0:shared].bitcast(BF16).rearrange("p t (n two) -> p n t two", two=2)
+                    into = upper[:, 0 : shared * PACK].rearrange("p (n t) -> p n t", t=PACK)
+                    nc.gpsimd.tensor_scalar(into, pairs[:, :, :, 1], 1.0, 0.0, ALU.mult, ALU.add)
+                halves = raw[a][:, :, first + shared : end].bitcast(BF16).rearrange("p t (g i two) -> p g t i two", i=4, two=2)
+                nc.scalar.copy(grouped(upper[:, shared * PACK :]), halves[:, :, :, :, 1])
                 nc.vector.tensor_scalar(hi[:, first * PACK : end * PACK].bitcast(I32), upper[:].bitcast(I32), HI_MASK, None, ALU.bitwise_and)
             return hi
 
@@ -185,7 +190,8 @@ def tile_list_tabgate_gelu_kernel(tc, tab_words, tab_scales, w, gT, b, offs, out
                 cut_lo(a, half, hi, lo[:, half * HALF : (half + 1) * HALF])
             cut = S if a == 0 else S // 2
             for start in range(0, S, cut):
-                gather_words(a, start, keep.tile([P, cut], U32, name="words%d_%d" % (a, start), align_bytes=64))
+                tag = "upper0_0" if a == 0 else "words%d_%d" % (a, start)
+                gather_words(a, start, keep.tile([P, cut], U32, name="words", tag=tag, align_bytes=64))
             hi = cut_hi(a + 1)
             quantise("upper%d_0" % (a + 1), lo, a, 1, 0)
             quantise("codes_hi%d" % (a + 1), hi, a + 1, 0, 0)

from contextlib import ExitStack

import concourse.mybir as mybir
from concourse.masks import make_identity

K, M, T, S = 1536, 512, 4096, 2048
FLOPS = 2 * 2 * K * M * S

F32 = mybir.dt.float32
BF16 = mybir.dt.bfloat16
I32 = mybir.dt.int32
U32 = mybir.dt.uint32
U16 = mybir.dt.uint16
U8 = mybir.dt.uint8
FP8X4 = mybir.dt.float8_e4m3fn_x4
ALU = mybir.AluOpType
GELU = mybir.ActivationFunctionType.Gelu_apprx_tanh

P = 128
PACK = 4
PASSES = K // (P * PACK)
TILES = M // P
OPEN = 2
BANK = 512
SLICES = S // BANK
BLOCK = P * PACK
HALF = 2 * BLOCK
HI_MASK = 0xFFF0FFF0 - (1 << 32)
LONG = 416
SCALE_ROWS = 16
SCALE_BASE = (32, 48, 112)
GATE_CUTS = [(1024, 1024), (2048,), (2048,), (1024, 640, 256, 128)]


def tile_list_tabgate_gelu_kernel(tc, tab_words, tab_scales, w, gT, b, offs, out):
    nc = tc.nc
    with ExitStack() as ctx:
        keep = ctx.enter_context(tc.tile_pool(name="keep", bufs=1))
        ring = ctx.enter_context(tc.tile_pool(name="ring", bufs=2))
        moved = ctx.enter_context(tc.tile_pool(name="moved", bufs=1))
        psum = ctx.enter_context(tc.psum_pool(name="psum", bufs=8))

        offsets = keep.tile([P, S // 16], U16, name="offsets")
        nc.sync.dma_start(offsets[:], offs)

        def picks(start, count):
            return offsets[:, start // 16 : (start + count) // 16]

        scale_rows = keep.tile([P, T // 4], I32, name="scale_rows", align_bytes=64)
        nc.vector.memset(scale_rows[0:32, :], 0)
        nc.gpsimd.memset(scale_rows[64:112, :], 0)
        flat_scales = tab_scales.rearrange("a q t -> (a q) t").bitcast(I32)
        nc.sync.dma_start(scale_rows[32:64, :], flat_scales[0:32, :])
        nc.sync.dma_start(scale_rows[112:128, :], flat_scales[32:48, :])
        raw = [keep.tile([P, PACK, M], F32, name="raw", tag="raw%d" % a) for a in range(PASSES)]

        def weight_rows(a):
            return w[BLOCK * a : BLOCK * (a + 1), :].rearrange("(p t) n -> p t n", t=PACK)

        tables = [keep.tile([P, T], I32, name="table", tag="table%d" % a, align_bytes=64) for a in range(PASSES)]

        def table_rows(a):
            return tab_words[a].rearrange("p t i -> p (t i)").bitcast(I32)

        planes = []
        for a in range(PASSES):
            planes.append(keep.tile([P, S // 4], I32, name="plane%d" % a, align_bytes=64))
            nc.gpsimd.memset(planes[a][:], 0)

        bias_rows = keep.tile([P, P], F32, name="bias_rows")
        nc.gpsimd.memset(bias_rows[0 : P - TILES, :], 0.0)
        identity = keep.tile([P, P], F32, name="identity")
        make_identity(nc, identity[:])

        picked_scales = moved.tile([P, S], U8, name="picked_scales", offset=0, align_bytes=64)
        nc.vector.tensor_copy(picked_scales[:], scale_rows[:].bitcast(U8).indirect(offsets[:]))

        def lay_scales(moves):
            for a, i in moves:
                base = SCALE_BASE[a]
                nc.sync.dma_start(planes[a][4 * a + i : P : 32, :], picked_scales[:].bitcast(I32)[base + i : base + SCALE_ROWS : 4, :])

        nc.sync.dma_start(raw[0][:], weight_rows(0))
        nc.sync.dma_start(tables[0][:], table_rows(0))
        nc.sync.dma_start(bias_rows[P - TILES : P, :], b.rearrange("(c p) -> c p", p=P))
        turned = psum.tile([P, P], F32, name="turned", tag="acc")
        nc.tensor.transpose(turned[:], bias_rows[:], identity[:])
        bias = keep.tile([P, TILES], F32, name="bias")
        nc.scalar.copy(bias[:], turned[:, P - TILES : P])
        nc.sync.dma_start(raw[1][:], weight_rows(1))
        lay_scales([(0, 0), (1, 0), (0, 1), (1, 1), (0, 2), (0, 3)])
        nc.sync.dma_start(tables[1][:], table_rows(1))
        nc.sync.dma_start(raw[2][:], weight_rows(2))
        lay_scales([(1, 2), (2, 0), (1, 3)])
        nc.sync.dma_start(tables[2][:], table_rows(2))
        lay_scales([(2, 1), (2, 2), (2, 3)])
        gates = []
        for m in range(TILES):
            gates.append(keep.tile([P, T], F32, name="gates", tag="gates%d" % m))
            nc.sync.dma_start(gates[m][:], gT[P * m : P * (m + 1), :])

        picked, weights = {}, {}

        def grouped(ap):
            return ap.rearrange("p (g i t) -> p g t i", i=4, t=PACK)

        def cut_hi(a):
            hi = keep.tile([P, TILES * BLOCK], BF16, name="hi%d" % a, align_bytes=64)
            for first, end in ([(0, M)] if a == 0 else [(0, LONG), (LONG, M)]):
                upper = keep.tile([P, (end - first) * PACK], BF16, name="upper", tag="upper%d_%d" % (a, first), align_bytes=64)
                shared = M // 2 if a == 0 else 0
                if shared:
                    pairs = raw[a][:, :, 0:shared].bitcast(BF16).rearrange("p t (n two) -> p n t two", two=2)
                    into = upper[:, 0 : shared * PACK].rearrange("p (n t) -> p n t", t=PACK)
                    nc.gpsimd.tensor_scalar(into, pairs[:, :, :, 1], 1.0, 0.0, ALU.mult, ALU.add)
                halves = raw[a][:, :, first + shared : end].bitcast(BF16).rearrange("p t (g i two) -> p g t i two", i=4, two=2)
                nc.scalar.copy(grouped(upper[:, shared * PACK :]), halves[:, :, :, :, 1])
                nc.vector.tensor_scalar(hi[:, first * PACK : end * PACK].bitcast(I32), upper[:].bitcast(I32), HI_MASK, None, ALU.bitwise_and)
            return hi

        def cut_lo(a, half, hi, lo):
            woven = keep.tile([P, HALF], F32, name="woven", tag="woven%d" % half, align_bytes=64)
            nc.scalar.copy(
                woven[:].rearrange("p (n t) -> p n t", t=PACK),
                raw[a][:, :, half * 2 * P : (half + 1) * 2 * P].rearrange("p t n -> p n t"),
            )
            nc.gpsimd.tensor_tensor(lo, woven[:], hi[:, half * HALF : (half + 1) * HALF], ALU.subtract)

        def quantise(tag, source, a, part, first, pool=keep, offset=None):
            count = source.shape[1] // BLOCK
            if offset is None:
                codes = keep.tile([P, count * P], U32, name="codes", tag=tag, align_bytes=64)
            else:
                codes = moved.tile([P, count * P], U32, name=tag, offset=offset, align_bytes=64)
            scales = keep.tile([P, count * P], U8, name="scales_" + tag, align_bytes=64)
            nc.vector.quantize_mx(codes[:].bitcast(FP8X4), scales[:], source[:, :])
            for place in range(count):
                weights[a, first + place, part] = (codes, scales, place * P)

        def gather_words(a, start, words):
            count = words.shape[1]
            nc.vector.tensor_copy(words[:, :], tables[a][:].bitcast(U32).indirect(picks(start, count)))
            for s in range(count // BANK):
                picked[a, start // BANK + s] = words[:, s * BANK : (s + 1) * BANK]

        accs, acts = {}, {}

        def multiply(a, part, m, s):
            if (a, part) == (0, 0):
                accs[m, s] = psum.tile([P, BANK], F32, name="acc")
            codes, scales, col = weights[a, m, part]
            nc.tensor.matmul_mx(
                out=accs[m, s][:],
                lhsT=codes[:, col : col + P].bitcast(FP8X4),
                lhsT_scale=scales[:, col : col + P],
                rhs=picked[a, s].bitcast(FP8X4),
                rhs_scale=planes[a][:].bitcast(U8)[4 * a : P, s * BANK : (s + 1) * BANK],
                start=(a, part) == (0, 0),
                stop=(a, part) == (PASSES - 1, 1),
            )

        def activate(m, s):
            if s == 0:
                acts[m] = ring.tile([P, S], F32, name="act")
            nc.scalar.activation(acts[m][:, s * BANK : (s + 1) * BANK], accs[m, s][:], GELU, bias=bias[:, m : m + 1])

        def gate(m):
            if m < OPEN:
                result = first_results[:, m, :]
            else:
                result = keep.tile([P, S], F32, name="result", tag="raw%d" % (m - OPEN))
            start = 0
            for count in GATE_CUTS[m]:
                cols = slice(start, start + count)
                nc.vector.tensor_tensor(result[:, cols], gates[m][:].indirect(picks(start, count)), acts[m][:, cols], ALU.mult)
                if m == TILES - 1:
                    nc.sync.dma_start(out[P * m : P * (m + 1), cols], result[:, cols])
                start += count
            if m == OPEN - 1:
                nc.sync.dma_start(out[0 : OPEN * P, :].rearrange("(m p) j -> p m j", p=P), first_results[:])
            if m == OPEN:
                nc.sync.dma_start(out[P * m : P * (m + 1), :], result[:])

        hi = cut_hi(0)
        quantise("codes_hi0", hi, 0, 0, 0)
        lo = hi
        last = PASSES - 1
        for a in range(last):
            for half in range(2):
                cut_lo(a, half, hi, lo[:, half * HALF : (half + 1) * HALF])
            cut = S if a == 0 else S // 2
            for start in range(0, S, cut):
                tag = "upper0_0" if a == 0 else "words%d_%d" % (a, start)
                gather_words(a, start, keep.tile([P, cut], U32, name="words", tag=tag, align_bytes=64))
            hi = cut_hi(a + 1)
            quantise("upper%d_0" % (a + 1), lo, a, 1, 0)
            quantise("codes_hi%d" % (a + 1), hi, a + 1, 0, 0)

        spare = lo
        cut_lo(last, 0, hi, spare[:, BLOCK : BLOCK + HALF])
        gather_words(last, 0, keep.tile([P, S // 2], U32, name="words_early", align_bytes=64))
        for m in range(OPEN):
            quantise("codes_lo_early%d" % m, spare[:, (m + 1) * BLOCK : (m + 2) * BLOCK], last, 1, m, offset=m * P * PACK)
        lo = spare[:, 0:HALF]
        cut_lo(last, 1, hi, lo)
        late = moved.tile([P, S // 2], U32, name="words_late", offset=S // 2, align_bytes=64)
        for s in range(2):
            gather_words(last, (2 + s) * BANK, late[:, s * BANK : (s + 1) * BANK])
        quantise("codes_lo_late", lo, last, 1, OPEN)

        for a in range(last):
            for part in range(2):
                for s in range(SLICES):
                    for m in range(OPEN):
                        multiply(a, part, m, s)

        def finish(m, s):
            for part in range(2):
                multiply(last, part, m, s)
            activate(m, s)

        def begin(m, s):
            for a in range(last):
                for part in range(2):
                    multiply(a, part, m, s)

        for m in range(OPEN):
            for s in range(SLICES // 2):
                finish(m, s)
        for s in range(SLICES // 2, SLICES):
            for m in range(OPEN):
                finish(m, s)
        first_results = keep.tile([P, OPEN, S], F32, name="first_results", tag="table0", align_bytes=64)
        for m in range(TILES):
            if m >= OPEN:
                for s in range(SLICES):
                    begin(m, s)
                    finish(m, s)
            gate(m)
